import numpy as np, ml_dtypes
CORES = [40,41,42,43,44,45,46,47]
N = 8
BF = ml_dtypes.bfloat16
def gentries(a):
    return np.ascontiguousarray(a.reshape(8, 16, -1).transpose(0, 2, 1)).reshape(8, -1)
def gtable(e):
    e = np.asarray(e); return np.ascontiguousarray(e.reshape(8, -1, 16).transpose(0, 2, 1)).reshape(128, -1).astype(np.int32)
V, A, VIS, ST = 3072, 256, 4, 3
def order(rng):
    return np.argsort(rng.random((N, 8, V)), axis=-1)
def by_order(o, ix):
    n = np.take_along_axis(o, ix.reshape(N, 8, V * 16), 2).reshape(N, 8, V, 16); b = np.empty_like(n)
    np.put_along_axis(b, o[..., None], n, 2)
    return b
def parts(rng):
    o = order(rng); i = np.arange(V)[None, None, :, None]; sh = (N, 8, V, 16)
    near = (i + rng.integers(-12, 13, sh)) % V; far = np.minimum((V * rng.random(sh) ** 2).astype(np.int64), V - 1)
    nm = by_order(o, np.where(rng.random(sh) < 0.5, near, far))
    return nm, rng.integers(0, 16, (N, 8, 16, V)), rng.integers(0, V, (N, 8, A)), rng.integers(0, 16, (N, 8, 16, A)), rng.integers(0, 32, (N, 8, 16, A))
def pack(nm, x, v, z, nz):
    return {"adj": np.stack([gtable(a.reshape(8, -1)) for a in nm]), "x": x.reshape(N, 128, V).astype(np.float32).astype(BF), "v0": np.stack([gtable(a) for a in v]),
            "z": z.reshape(N, 128, A).astype(np.float32).astype(BF), "nz": nz.reshape(N, 128, A).astype(np.float32).astype(BF)}
def setup_inputs(rng):
    return pack(*parts(rng))
def setup_inputs_loops(rng):
    nm, x, v, z, nz = parts(rng); o = order(rng); i = np.arange(V)[None, None, :]; m = ST + 1
    chain = np.where(i % m == m - 1, i - i % m + rng.integers(0, m, (N, 8, V)), (i + 1) % V)
    c = rng.integers(2, 3 * ST, (N, 8, 1)); base = i - i % c
    circle = np.minimum(base[..., None] + (rng.random((N, 8, V, 16)) * c[..., None]).astype(np.int64), V - 1)
    odd = (np.arange(8) % 2 == 1)[None, :, None, None]
    nm = by_order(o, np.where(odd, circle, chain[..., None]))
    alike = np.take_along_axis(x, np.take_along_axis(o, base, 2)[:, :, None, :], 3); y = np.empty_like(x)
    np.put_along_axis(y, o[:, :, None, :], alike, 3)
    return pack(nm, np.where(odd, y, x), v, z, nz)
def setup_inputs_crowd(rng):
    nm, x, v, z, nz = parts(rng); h = 12
    hub = 1 + np.argsort(rng.random((8, V - 2)), axis=-1)[:, :h]; hub[:, 0] = 0; hub[:, 1] = V - 1
    for g in range(6):
        for q in range(N):
            nm[q, g, hub[g]] = hub[g][rng.integers(0, h, (h, 16))]
        v[:, g] = hub[g][rng.integers(0, h, (N, A))]
    for q in range(N):
        p = rng.permutation(h); nm[q, 5, hub[5][p], 3] = hub[5][np.roll(p, -1)]
    x[:, 5] = x[:, 5, :, :1]; nz[:, 5] = 0; nz[:, 5, 3] = 31
    v[:, 6] = V - 1; v[:, 7] = 0
    return pack(nm, x, v, z, nz)
def setup_inputs_ties(rng):
    nm, x, v, z, nz = parts(rng)
    x[:, :2] = 7 + x[:, :2] % 2; z[:, :2] = 7 + z[:, :2] % 2; nz[:, :2] = nz[:, :2] % 2
    x[:, 2:4] = 15 * (x[:, 2:4] % 2); z[:, 2:4] = 15 * (z[:, 2:4] % 2); nz[:, 2:4] = 0
    v[:, 2, 0] = 0; nm[:, 2, 0] = V - 1; x[:, 2, :, V - 1] = 15; z[:, 2, :, 0] = 0
    x[:, 4] = 5; nz[:, 4] = 30 + nz[:, 4] % 2
    x[:, 5] = x[:1, 5]; nm[:, 5] = nm[:1, 5]; nz[:, 5] = 0
    nm[:, 6] = np.tile(nm[:, 6, :, :2], (1, 1, 8)); nz[:, 6] = nz[:, 6] % 4
    nz[:, 7] = 31
    return pack(nm, x, v, z, nz)
def setup_inputs_ends(rng):
    nm, x, v, z, nz = parts(rng)
    x[:, 0] = 15 - (x[:, 0] == 0).astype(np.int64); z[:, 0] = 0; nz[:, 0] = nz[:, 0] % 2
    x[:, 4] = (x[:, 4] == 0).astype(np.int64); z[:, 4] = 15; nz[:, 4] = nz[:, 4] % 4
    x[:, 1] = 7 + (x[:, 1] == 0).astype(np.int64); z[:, 1] = 7; nz[:, 1] = 24 + nz[:, 1] % 8
    level = ((int(rng.integers(0, N)) - np.arange(N)) % N)[:, None, None]
    x[:, 2] = 2 * level + x[:, 2] % 2; x[:, 3] = 2 * level; z[:, 2:4] = 0
    i = np.arange(V)[None, None, :, None]
    nm[:, 2:4] = by_order(order(rng), (i + 1 + rng.integers(0, 13, (N, 8, V, 16))) % V)[:, 2:4]
    v[:, 2:4] = np.argsort(rng.random((N, 2, V)), axis=-1)[..., :A]; v[:, 3, A - 1] = v[:, 3, 0]
    nz[:, 3] = nz[:, 3] % 31
    for q in range(N):
        k = int(rng.integers(0, 16)); nz[q, 3, k, 0] = 31; nz[q, 3, (k + 1 + int(rng.integers(0, 15))) % 16, A - 1] = 31
    return pack(nm, x, v, z, nz)
def setup_inputs_spread(rng):
    nm, x, v, z, nz = parts(rng); e = np.array([0.5, 1.0, 2.0, 4.0])
    ix = np.minimum(np.exp2(np.log2(V) * rng.random((N, 8, V, 16))).astype(np.int64) - 1, V - 1)
    nm = by_order(order(rng), ix); nm[:, 1::2] = V - 1 - ix[:, 1::2]
    x = np.minimum((16 * rng.random(x.shape) ** rng.choice(e, (N, 8, 1, V))).astype(np.int64), 15)
    z = np.minimum((16 * rng.random(z.shape) ** rng.choice(e, (N, 8, 1, A))).astype(np.int64), 15)
    nz = np.minimum((32 * rng.random(nz.shape) ** rng.choice(e, (N, 8, 16, 1))).astype(np.int64), 31)
    v = np.minimum((V * rng.random(v.shape) ** rng.choice(e, (N, 8, 1))).astype(np.int64), V - 1)
    return pack(nm, x, v, z, nz)
def check_inputs(d):
    bad = []
    for k, hi in (("adj", V - 1), ("v0", V - 1)):
        if np.min(d[k]) < 0 or np.max(d[k]) > hi: bad.append("range of " + k)
    for k, hi in (("x", 15), ("z", 15), ("nz", 31)):
        b = np.asarray(d[k]).astype(np.float32)
        if not np.all((b >= 0) & (b <= hi) & (b == np.floor(b))): bad.append("whole numbers of " + k)
    return bad
def reference(adj, x, v0, z, nz):
    nm = np.stack([gentries(b) for b in adj]).astype(np.int64).reshape(N, 8, V, 16)
    xt = np.ascontiguousarray(x.astype(np.float32).astype(np.int32).reshape(N, 8, 16, V).transpose(0, 1, 3, 2))
    w = np.ascontiguousarray(z.astype(np.float32).astype(np.int32).reshape(N, 8, 16, A).transpose(0, 1, 3, 2))
    no = np.ascontiguousarray(nz.astype(np.float32).astype(np.int64).reshape(N, 8, 16, A).transpose(0, 1, 3, 2))
    v = np.stack([gentries(b) for b in v0]).astype(np.int64)
    ph = np.full((N, 8, V, 16), 8, np.int64)
    r = np.arange(N)[:, None, None]; g = np.arange(8)[None, :, None]; pl = np.arange(ST)
    oldn = oldk = oldd = None
    for i in range(VIS):
        if i > 0: v = np.roll(v, 1, axis=0); w = np.roll(w, 1, axis=0)
        tn = np.full((N, 8, A, ST), -1, np.int64); tk = np.zeros((N, 8, A, ST), np.int64); ln = np.zeros((N, 8, A), np.int64)
        for s in range(ST):
            names = nm[r, g, v]
            far = np.sum(np.abs(xt[r[..., None], g[..., None], names] - w[:, :, :, None, :]), axis=4)
            k = np.argmax(ph[r, g, v] + np.roll(no, -(i * ST + s), axis=2) - far, axis=3)
            nv = np.take_along_axis(names, k[..., None], 3)[..., 0]
            here = pl == ln[..., None]
            tn = np.where(here, v[..., None], tn); tk = np.where(here, k[..., None], tk)
            hit = tn == nv[..., None]
            ln = np.where(np.any(hit, axis=3), np.argmax(hit, axis=3), ln + 1)
            tn = np.where(pl < ln[..., None], tn, -1); v = nv
        dd = np.sum(np.abs(xt[r, g, v] - w), axis=3)
        if i > 0:
            better = np.roll(dd < np.roll(oldd, 1, axis=0), -1, axis=0)
            for p in range(ST):
                q, h, b = np.nonzero(better & (oldn[..., p] >= 0))
                n = oldn[q, h, b, p]; kk = oldk[q, h, b, p]
                low = np.full((N, 8, V), A, np.int64); np.minimum.at(low, (q, h, n), b)
                m = low[q, h, n] == b; q, h, n, kk = q[m], h[m], n[m], kk[m]
                was = ph[q, h, n]; now = np.maximum(was - 3, 0); j = np.arange(len(q))
                now[j, kk] = np.minimum(was[j, kk] + 8, 20)
                ph[q, h, n] = now
        oldn, oldk, oldd = tn, tk, dd
    return {"yp": ph.transpose(0, 1, 3, 2).reshape(N, 128, V).astype(np.float32).astype(BF), "yv": np.stack([gtable(b) for b in v]).astype(np.float32)}

@@ -1,0 +1,504 @@
+import numpy as np
+from concourse.bass import DstId, RemoteDMATransfer
+from concourse.mybir import AluOpType as ALU, ActivationFunctionType as ACT
+
+V, A, VIS, ST = 3072, 256, 4, 3
+CEN = 1536.0
+SC1 = 65536.0
+NV = [[64, 64, 64], [64, 64, 64], [16, 64, 64], [16, 64, 64]]
+VPIECE, SPIECE = 32, 32
+F32, BF, F16, I32, U16 = "float32", "bfloat16", "float16", "int32", "uint16"
+
+_SB = {
+    "adjs": (V, I32), "xs": (V, BF), "ph": (V + 32, BF), "v0s": (16, I32), "zs": (A, BF), "nzs": (A, BF), "nzk": (A + 16, F16),
+    "rr": (256, F32), "rm": (256, F32), "rg": (128, F32), "rq": (40, F32), "pi": (8, I32), "pf": (16, F32),
+    "ib": (128, BF), "ih": (128, F16), "i65": (256, BF), "i16": (128, BF), "i4k": (256, F16), "c1": (16, BF), "c2": (16, BF),
+    "rst": (256, F32), "sel": (240, F16), "xm": (128, F16), "b0": (144, BF), "jc": (16, F32), "lc": (16, F32),
+    "seld": (2048, F16), "lall": (2048, BF), "dtab": (16, BF), "elf": (40, F32), "el": (40, U16), "dm": (144, F32),
+    "wn": (48, I32), "w2": (72, I32), "ki": (64, I32), "k2": (32, I32), "ek": (384, F16),
+    "n16": (64, F32), "pp": (48, F32), "ne": (128, F32), "dd": (48, F32), "ff": (48, F32), "fi": (48, I32), "uk": (96, I32),
+    "val": (48, F32), "ww": (48, F32), "oc": (72, F16), "on": (72, F16), "eq": (1152, BF), "off": (48, U16),
+    "new": (256, BF), "yvs": (16, F32),
+}
+for _i in range(VIS):
+    _SB.update({"zr%d" % _i: (16 * A, BF), "vl%d" % _i: (64, U16), "dn%d" % _i: (16, BF)})
+    if _i > 0:
+        _SB["bt%d" % _i] = (48, BF)
+    if _i < VIS - 1:
+        _SB.update({"ul%d" % _i: (96, U16), "d3%d" % _i: (48, BF), "ud%d" % _i: (48, F32), "dl%d" % _i: (768, BF)})
+for _b in range(2):
+    _SB.update({"nm%d" % _b: (128, U16), "nf%d" % _b: (128, F16), "pg%d" % _b: (128, BF), "a1%d" % _b: (2048, BF),
+                "a2%d" % _b: (2048, BF), "sc%d" % _b: (256, F32), "e1%d" % _b: (128, F16)})
+SCRATCH = {_n: ("sbuf", [128, _w], _d) for _n, (_w, _d) in _SB.items()}
+for _n in ("pk0", "pk1", "pd0", "pd1", "pd2", "pe0", "pe1", "phop"):
+    SCRATCH[_n] = ("psum", [128, 512], F32)
+
+SEMAPHORES = (["cV", "cS", "cP", "cG", "sent", "l_adj", "l_x", "l_v", "l_z", "l_nz", "o_p", "o_v"]
+              + ["r_z%d" % i for i in (1, 2, 3)]
+              + ["r_%s%d%d" % (k, i, b) for k in "vf" for i in (1, 2, 3) for b in (0, 1)])
+
+CY, GA, SCT, PC, HOP = 1.0, 1.56, 3.8, 0.5, 90.0
+NS, RS, TS = 2.0, 5.5, 8.5
+
+
+def _v(n, c=1.0):
+    return max(64.0, n * c) * CY
+
+
+def _ga(n):
+    return 60.0 + n * GA * CY
+
+
+def _build(g, T, topo, core, rank):
+    ops = []
+    last_w, readers = {}, {}
+    slot = [-9.0]
+    nxt, prv = T.cores[(rank + 1) % len(T.cores)], T.cores[(rank - 1) % len(T.cores)]
+    vec, sca, pe = g.vector, g.scalar, g.tensor
+
+    def add(eng, fn, cost, r=(), w=(), x=(), sem=None, lat=0.0, after=()):
+        n = len(ops)
+        deps = {}
+        for d in after:
+            deps[d] = True
+        for k in r:
+            if k in last_w:
+                deps[last_w[k]] = True
+        for k in tuple(w) + tuple(x):
+            for d in ([last_w[k]] if k in last_w else []) + readers.get(k, []):
+                deps[d] = deps.get(d, False) or ops[d]["eng"] != eng or k not in x
+        for k in r:
+            readers.setdefault(k, []).append(n)
+        for k in tuple(w) + tuple(x):
+            last_w[k] = n
+            readers[k] = []
+        deps.pop(n, None)
+        ops.append({"eng": eng, "fn": fn, "cost": cost, "deps": deps, "sem": sem, "lat": lat, "slot": slot[0],
+                    "w": (tuple(w) + tuple(x))[:1]})
+        return n
+
+    def ts(out, in0, s1, s2, o0, o1, n, r, w, c=1.0, x=()):
+        if o1 is None:
+            return add("V", lambda: vec.tensor_scalar(out, in0, s1, None, o0), _v(n, c), r, w, x)
+        return add("V", lambda: vec.tensor_scalar(out, in0, s1, s2, o0, o1), _v(n, c), r, w, x)
+
+    def tt(out, a, b, op, n, r, w, x=()):
+        return add("V", lambda: vec.tensor_tensor(out, a, b, op), _v(n, 1.0 if x else 2.0), r, w, x)
+
+    def cp(out, a, n, r, w, x=(), cost=None):
+        return add("V", lambda: vec.tensor_copy(out, a), cost or _v(n), r, w, x)
+
+    def mm(lst, r, x):
+        def fn():
+            ins = None
+            for (o, l, rh, st, sp) in lst:
+                ins = pe.matmul(o, l, rh, st, sp)
+            return ins
+        return add("P", fn, sum(max(64, q[0].shape[-1]) for q in lst) * PC, r, (), x)
+
+    def dst(c):
+        rid, pid, _ = topo.addr(c)
+        return DstId(rid=rid, pnc=pid)
+
+    def bits(es):
+        return sum(1 << e for e in es)
+
+    nsent = [0]
+
+    def send(trs, r, lat, after=()):
+        nsent[0] += sum(len(t[3]) for t in trs)
+
+        def fn():
+            g.remote_dma_fused([RemoteDMATransfer(dst_ids=[dst(c)] * len(d), dma_engine_mask=bits(es), remote_sem=T.sem[sem],
+                                                  srcs=[s], dsts=d) for (c, s, d, es, sem, w) in trs], local_sem=T.sem.sent)
+            return None
+        n = add("G", fn, 300.0, r, (), after=after)
+        for (c, s, d, es, sem, w) in trs:
+            add(None, None, 0.0, (), w, sem=(sem, len(es) * len(d)), lat=lat, after=(n,))
+
+    def load(q, eng, out, in_, name, sem, lat):
+        return add(eng, lambda: q.dma_start(out, in_), 100.0, (), (name,), sem=(sem, 16), lat=lat)
+    load(g.sync, "Y", T.zs[:], T.z[:], "zs", "l_z", 2500.0)
+    load(sca, "S", T.v0s[:], T.v0[:], "v0s", "l_v", 2500.0)
+    la = load(g.sync, "Y", T.adjs[:], T.adj[:], "adjs", "l_adj", 8000.0)
+    load(sca, "S", T.nzs[:], T.nz[:], "nzs", "l_nz", 3000.0)
+    lx = load(sca, "S", T.xs[:], T.x[:], "xs", "l_x", 8000.0)
+
+    def iota(out, pat, name, n):
+        add("G", lambda: g.iota(out, pat, 0, 0, allow_small_or_imprecise_dtypes=True), 130.0 + 2 * n, (), (name,))
+    add("G", lambda: g.iota(T.pi[:, 0:1], [[0, 1]], 0, 1), 130.0, (), ("pi0",))
+    iota(T.rr[:], [[1, 256]], "rr", 256)
+    iota(T.rm[:], [[0, 16], [1, 16]], "rm", 256)
+    iota(T.rg[:], [[1, 8], [0, 16]], "rg", 128)
+    iota(T.rq[:, 0:24], [[1, 8], [16, 3]], "rq0", 24)
+    iota(T.rq[:, 24:40], [[0, 2], [1, 8]], "rq1", 16)
+    AND, SHR = ALU.bitwise_and, ALU.logical_shift_right
+    ts(T.pi[:, 1:2], T.pi[:, 0:1], 15, None, AND, None, 1, ("pi0",), ("pi1",))
+    ts(T.pi[:, 2:3], T.pi[:, 0:1], 4, None, SHR, None, 1, ("pi0",), ("pi2",))
+    ts(T.pi[:, 3:4], T.pi[:, 0:1], 7, None, AND, None, 1, ("pi0",), ("pi3",))
+    ts(T.pi[:, 4:5], T.pi[:, 0:1], 3, 1, SHR, AND, 1, ("pi0",), ("pi4",))
+    cp(T.pf[:, 0:5], T.pi[:, 0:5], 5, ("pi0", "pi1", "pi2", "pi3", "pi4"), ("pf",))
+    P, PM, PG, P7, HB, COND, KK, DUM, DUC, HB1, HB8, G16, DUO, HB2 = (T.pf[:, k:k + 1] for k in range(14))
+    tt(COND, P7, PG, ALU.is_equal, 1, ("pf",), ("cond",))
+    for (col, src, m, a, name) in ((KK, PM, -1.0, 15.0, "kk"), (DUM, PM, 1.0, float(V), "dum"), (DUC, PM, 1.0, V - CEN, "duc"),
+                                   (DUO, PM, 1.0, V - CEN + 16, "duo"), (HB1, HB, 1.0, -16.0, "hb1"), (HB2, HB, 8.0, -16.0, "hb2"),
+                                   (HB8, HB, 8.0, -64.0, "hb8"), (G16, PG, 16.0, 16.0, "g16")):
+        ts(col, src, m, a, ALU.mult, ALU.add, 1, ("pf",), (name,))
+    ts(T.ib[:], T.rr[:, 0:128], P, None, ALU.is_equal, None, 128, ("rr", "pf"), ("ib",))
+    for (out, m, name) in ((T.ih[:], 1.0, "ih"), (T.i4k[:, 0:128], 4096.0, "i4k0"), (T.i4k[:, 128:256], 4096.0, "i4k1"),
+                           (T.i65[:, 0:128], SC1, "i650"), (T.i65[:, 128:256], SC1, "i651"), (T.i16[:], 16.0, "i16")):
+        ts(out, T.ib[:], m, None, ALU.mult, None, 128, ("ib",), (name,), 0.5)
+    ts(T.c1[:], T.rq[:, 24:40], PG, -2.0 * SC1, ALU.is_equal, ALU.mult, 16, ("rq1", "pf"), ("c1",))
+    ts(T.c2[:], T.rq[:, 24:40], PG, SC1, ALU.is_equal, ALU.mult, 16, ("rq1", "pf"), ("c2",))
+    ts(T.rst[:], T.rm[:], 0.0, -67108864.0, ALU.is_equal, ALU.mult, 256, ("rm",), ("rst",))
+    ts(T.sel[:], T.rr[:, 0:240], PM, 112.0, ALU.subtract, ALU.is_equal, 240, ("rr", "pf"), ("sel",))
+    ts(T.nzk[:, 0:A], T.nzs[:], 16.0, KK, ALU.mult, ALU.add, A, ("nzs", "kk"), ("nzk0",), 0.5)
+    ts(T.nzk[:, A:A + 16], T.nzs[:, 0:16], 16.0, KK, ALU.mult, ALU.add, 16, ("nzs", "kk"), ("nzk1",))
+    ts(T.elf[:, 0:4], T.rr[:, 0:8:2], HB1, COND, ALU.add, ALU.mult, 4, ("rr", "hb1", "cond"), ("elf0",))
+    ts(T.elf[:, 4:12], T.rr[:, 0:8], HB2, COND, ALU.add, ALU.mult, 8, ("rr", "hb2", "cond"), ("elf1",))
+    ts(T.el[:, 0:12], T.elf[:, 0:12], 16.0, None, ALU.add, None, 12, ("elf0", "elf1"), ("el0",))
+    ts(T.rq[:, 2:24:3], T.rq[:, 2:24:3], HB8, 64.0, ALU.add, ALU.add, 8, ("rq0", "hb8"), ("rq0",))
+    ts(T.elf[:, 12:36], T.rq[:, 0:24], HB8, COND, ALU.add, ALU.mult, 24, ("rq0", "hb8", "cond"), ("elf2",))
+    ts(T.el[:, 12:36], T.elf[:, 12:36], 64.0, None, ALU.add, None, 24, ("elf2",), ("el1",))
+    add("V", lambda: vec.memset(T.wn[:], int(CEN)), _v(48), (), ("wn0", "wn1", "wd0", "wd1"))
+    add("V", lambda: vec.memset(T.w2[:], 0), _v(72), (), ("w2k",))
+    cp(T.vl0[:, 0:16], T.v0s[:], 16, ("v0s",), (("vl", 0, 0, 0), ("vl", 0, 0, 1)))
+    for k in range(16):
+        if k % 2:
+            add("S", lambda k=k: sca.activation(T.zr0[:, k::16], T.zs[:], ACT.Copy, scale=-1.0), 70.0 + A * CY, ("zs",), (("zr", 0, k),))
+        else:
+            ts(T.zr0[:, k::16], T.zs[:], -1.0, None, ALU.mult, None, A, ("zs",), (("zr", 0, k),), 0.5)
+    zall = {i: [("zr", i, 0)] for i in range(1, VIS)}
+    zall[0] = [("zr", 0, k) for k in range(16)]
+    for i in range(1, VIS):
+        c = T.cores[(rank + i) % len(T.cores)]
+        send([(c, T.zr0[:], [T["zr%d" % i][:]], topo.engines(core, c), "r_z%d" % i, zall[i])], zall[0], 5000.0 * i, after=(la, lx))
+    slot[0] = 6.5
+    phi = [("phi", q) for q in range(4)]
+    for q in range(4):
+        add("V", lambda q=q: vec.memset(T.ph[:, 776 * q:776 * q + 776], 8.0), _v(776, 0.5), (), (("phi", q),))
+    iota(T.dm[:, 0:48], [[0, 24], [16, 2]], "dm0", 48)
+    ts(T.dm[:, 48:96], T.dm[:, 0:48], DUM, None, ALU.add, None, 48, ("dm0", "dum"), ("dm1",))
+    ts(T.dm[:, 96:144], T.dm[:, 0:48], DUC, -1.0, ALU.add, ALU.mult, 48, ("dm0", "duc"), ("dm2",))
+    ts(T.dm[:, 0:48], T.dm[:, 0:48], DUC, None, ALU.add, None, 48, ("dm0", "duc"), ("dm0",))
+    ts(T.jc[:], T.rr[:, 0:16], PM, None, ALU.is_equal, None, 16, ("rr", "pf"), ("jc",))
+    ts(T.lc[:], T.rr[:, 0:16], PM, None, ALU.is_gt, None, 16, ("rr", "pf"), ("lc",))
+    ts(T.xm[:], T.rg[:], PG, None, ALU.is_equal, None, 128, ("rg", "pf"), ("xm",))
+    ts(T.b0[:], T.rr[:, 0:144], G16, 4096.0, ALU.is_equal, ALU.mult, 144, ("rr", "g16"), ("b0",))
+    for j in range(16):
+        ts(T.seld[:, 128 * j:128 * j + 128], T.xm[:], T.jc[:, j:j + 1], None, ALU.mult, None, 128, ("xm", "jc"), (("seld", j),), 0.5)
+        ts(T.lall[:, 128 * j:128 * j + 128], T.b0[:, 16 - j:144 - j], T.lc[:, j:j + 1], None, ALU.mult, None, 128,
+           ("b0", "lc"), (("lall", j),), 0.5)
+    ts(T.dtab[:], T.rr[:, 0:16], KK, 11.0, ALU.is_equal, ALU.mult, 16, ("rr", "kk"), ("dtab",))
+    ts(T.dtab[:], T.dtab[:], -3.0, None, ALU.add, None, 16, ("dtab",), ("dtab",))
+
+    def hop(out, e, nq, r, bank):
+        mm([(out, T.sel[:, 112 - 16 * c:240 - 16 * c], e[:, 8 * nq * c:8 * nq * (c + 1)], c == 0, c == 7) for c in range(8)],
+           tuple(r) + ("sel",), (bank,))
+
+    pcount = [0]
+
+    def step(i, s, b):
+        t = ST * i + s
+        last = s == ST - 1
+        nv = NV[i][s]
+        W = 256 if last else 128
+        vl, zr = T["vl%d" % i], T["zr%d" % i]
+        nm, nf, pg, a1, a2, sc, e1, pk = (T["%s%d" % (n, b)] for n in ("nm", "nf", "pg", "a1", "a2", "sc", "e1", "pk"))
+        bank = "pk%d" % b
+        lst = vl[:, 16 * s + 8 * b:16 * s + 8 * b + 8]
+        vn = ("vl", i, s, b)
+        nzl = T.nzk[:, 128 * b + t:128 * b + t + 128]
+        slot[0] = 2 * t + b - NS
+        cp(nm[:], T.adjs[:, 0:V].indirect(lst), 128, ("adjs", vn), (("nm", b),), cost=_ga(128))
+        slot[0] = 2 * t + b
+        ts(nf[:], nm[:], CEN, None, ALU.subtract, None, 128, (("nm", b),), (("nf", b),), 0.5)
+        mm([(pk[:, 0:W], nzl, T.i4k[:, 0:W], True, False)], ("nzk0", "nzk1", "i4k0", "i4k1"), (bank,))
+        a1n, a2n = [], []
+        for c0 in range(nv, 128, SPIECE):
+            c1 = min(128, c0 + SPIECE)
+            n = 16 * (c1 - c0)
+            pn = "pd%d" % (pcount[0] % 3)
+            pcount[0] += 1
+            pd = T[pn]
+            n1, n2 = [("a1", b, c) for c in range(c0, c1, 8)], [("a2", b, c) for c in range(c0, c1, 8)]
+            add("S", lambda c0=c0, c1=c1: sca.activation(a2[:, 16 * c0:16 * c1], T.xs[:, 0:V].indirect(nm[:, c0:c1]), ACT.Copy),
+                10.0 + _ga(n), ("xs", ("nm", b)), n2)
+            mm([(pd[:, 0:n], T.ib[:], zr[:, 2048 * b + 16 * c0:2048 * b + 16 * c1], True, False)], ["ib"] + zall[i], (pn,))
+            mm([(pd[:, 0:n], T.ib[:], a2[:, 16 * c0:16 * c1], False, True)], ["ib"] + n2, (pn,))
+            add("S", lambda c0=c0, c1=c1, pd=pd, n=n: sca.activation(a1[:, 16 * c0:16 * c1], pd[:, 0:n], ACT.Abs, scale=0.5),
+                70.0 + n * CY, (), n1, (pn,))
+            a1n += n1
+        for c0 in range(0, nv, VPIECE):
+            c1 = min(nv, c0 + VPIECE)
+            n = 16 * (c1 - c0)
+            n1, n2 = [("a1", b, c) for c in range(c0, c1, 8)], [("a2", b, c) for c in range(c0, c1, 8)]
+            add("V", lambda c0=c0, c1=c1: vec.tensor_tensor(a2[:, 16 * c0:16 * c1], T.xs[:, 0:V].indirect(nm[:, c0:c1]),
+                                                            zr[:, 2048 * b + 16 * c0:2048 * b + 16 * c1], ALU.add),
+                _ga(n), ["xs", ("nm", b)] + zall[i], n2)
+            ts(a1[:, 16 * c0:16 * c1], a2[:, 16 * c0:16 * c1], 0.0, None, ALU.max, None, n, n2, n1, 0.5)
+            a1n += n1
+            a2n += n2
+        if nv:
+            mm([(pk[0:nv, k:W:16], a2[:, k:16 * nv:16], T.c2[:, 0:W // 16], False, False) for k in range(16)], a2n + ["c2"], (bank,))
+        mm([(pk[:, k:W:16], a1[:, k:2048:16], T.c1[:, 0:W // 16], False, False) for k in range(16)], a1n + ["c1"], (bank,))
+        fin, rd = [], [("nf", b), "ih", "nzk0", "nzk1"]
+        if i >= 2:
+            add("S", lambda: sca.activation(pg[:], T.ph[:, 0:V].indirect(lst), ACT.Copy), 10.0 + _ga(128), ("ph", vn), (("pg", b),))
+            fin.append((pk[:, 0:W], pg[:], T.i65[:, 0:W], False, False))
+            rd += [("pg", b), "i650", "i651", "i16"]
+            if last:
+                fin.append((pk[:, 128:256], pg[:], T.i16[:], False, False))
+        if last:
+            fin.append((pk[:, 128:256], nzl, T.ih[:], False, False))
+        fin.append((pk[:, 0:128], nf[:], T.ih[:], False, True))
+        mm(fin, rd, (bank,))
+        add("V", lambda: vec.tensor_tensor_scan(sc[:, 0:W], T.rst[:, 0:W], pk[:, 0:W], 0.0, ALU.add, ALU.max), _v(W),
+            ("rst",), (("sc", b),), (bank,))
+        nq = 2 if last else 1
+        ko = 32 + 16 * b if last else 16 * s + 8 * b
+        wn = 24 * b
+        ts(T.ki[:, ko:ko + 8 * nq], sc[:, 15:W:16], CEN, None, ALU.add, None, 8, (("sc", b),), (("ki", s, b),))
+        ts(T.wn[:, wn:wn + 8], T.ki[:, ko:ko + 8], 4095, None, AND, None, 8, (("ki", s, b),), ("wn%d" % b,))
+        if last:
+            k2, ka, kc = T.ki[:, ko + 8:ko + 16], T.k2[:, 16 * b:16 * b + 8], T.k2[:, 16 * b + 8:16 * b + 16]
+            ts(ka, k2, 4095, 4, AND, SHR, 8, (("ki", s, b),), (("k2a", b),))
+            ts(kc, k2, 16, None, ALU.arith_shift_right, None, 8, (("ki", s, b),), (("k2c", b),))
+            tt(T.wn[:, wn + 8:wn + 16], ka, kc, ALU.subtract, 8, (("k2a", b), ("k2c", b)), ("wd%d" % b,))
+        el = T.el[:, 4:12] if last else T.el[:, 0:4]
+        add("V", lambda: vec.tensor_scalar(e1[:, 0:64 * nq], T.wn[:, wn:wn + 24].indirect(el), CEN, None, ALU.subtract),
+            _ga(64 * nq), ("wn%d" % b, "wd%d" % b, "el0"), (("e1", b),))
+        hop(pk[:, 256:256 + 8 * nq], e1, nq, (("e1", b),), bank)
+        o = 16 * (s + 1) + 8 * b
+        if last:
+            dn = T["dn%d" % i][:, 8 * b:8 * b + 8]
+            ts(dn, pk[:, 264:272], CEN - CEN / 16, None, ALU.add, None, 8, (), (("dn", i, b),), x=(bank,))
+        ts(vl[:, o:o + 8], pk[:, 256:264], CEN, None, ALU.add, None, 8, (), (("vl", i, s + 1, b),), x=(bank,))
+        if last:
+            trs, rd = [], []
+            e_n, e_p = topo.engines(core, nxt), topo.engines(core, prv)
+            if 0 < i < VIS - 1:
+                e_n, e_p = e_n[:len(e_n) // 2], e_p[len(e_p) // 2:]
+            if i < VIS - 1:
+                trs.append((nxt, vl[:, o:o + 8], [T["vl%d" % (i + 1)][:, 8 * b:8 * b + 8]], e_n, "r_v%d%d" % (i + 1, b), (("vl", i + 1, 0, b),)))
+                rd.append(("vl", i, s + 1, b))
+            if i > 0:
+                trs.append((prv, dn, [T["bt%d" % i][:, 16 * p + 8 * b:16 * p + 8 * b + 8] for p in range(3)], e_p,
+                            "r_f%d%d" % (i, b), (("bt", i, b),)))
+                rd.append(("dn", i, b))
+            send(trs, rd, 1800.0)
+
+    def trails(i):
+        slot[0] = 6 * i + 5
+        ts(T.w2[:, 0:64], T.ki[:], 12, 15, SHR, AND, 64, [("ki", s, b) for s in range(3) for b in range(2)], ("w2k",))
+        slot[0] = 6 * i + TS
+        cp(T.ek[:], T.w2[:, 0:72].indirect(T.el[:, 12:36]), 384, ("w2k", "el1"), ("ek",), cost=_ga(384))
+        hop(T.phop[:, 16:64], T.ek, 6, ("ek",), "phop")
+        for p in range(3):
+            cp(T["d3%d" % i][:, 16 * p:16 * p + 16], T["dn%d" % i][:], 16, (("dn", i, 0), ("dn", i, 1)), (("d3", i, p),))
+        n16, pp, ne, dd, ff, val = T.n16, T.pp, T.ne, T.dd, T.ff, T.val
+        ts(n16[:], T["vl%d" % i][:], 16.0, None, ALU.mult, None, 64, [("vl", i, s, b) for s in range(4) for b in range(2)], ("n16",))
+        tt(pp[:], T.phop[:, 16:64], n16[:, 0:48], ALU.add, 48, ("n16",), ("pp",), ("phop",))
+        tt(ne[:, 0:48], n16[:, 0:48], n16[:, 16:64], ALU.not_equal, 48, ("n16",), ("ne0", "nem"))
+        tt(ne[:, 48:80], n16[:, 0:32], n16[:, 32:64], ALU.not_equal, 32, ("n16",), ("ne1",))
+        tt(val[:, 0:16], n16[:, 0:16], n16[:, 48:64], ALU.not_equal, 16, ("n16",), ("val0",))
+        tt(ne[:, 16:32], ne[:, 0:16], ne[:, 16:32], ALU.mult, 16, ("ne0", "nem"), ("nem",))
+        tt(dd[:, 0:32], pp[:, 0:32], pp[:, 16:48], ALU.subtract, 32, ("pp",), ("dd",))
+        tt(ne[:, 80:96], ne[:, 48:64], ne[:, 64:80], ALU.mult, 16, ("ne1",), ("q",))
+        tt(dd[:, 0:32], dd[:, 0:32], ne[:, 0:32], ALU.mult, 32, ("dd", "ne0", "nem"), ("dd",))
+        tt(ne[:, 80:96], ne[:, 80:96], val[:, 0:16], ALU.mult, 16, ("q", "val0"), ("q",))
+        tt(ne[:, 96:112], ne[:, 16:32], ne[:, 32:48], ALU.max, 16, ("ne0", "nem"), ("x1",))
+        tt(ne[:, 112:128], ne[:, 16:32], ne[:, 32:48], ALU.min, 16, ("ne0", "nem"), ("x2",))
+        tt(ff[:, 0:32], pp[:, 16:48], dd[:, 0:32], ALU.add, 32, ("pp", "dd"), ("f0", "f1"))
+        tt(val[:, 16:32], ne[:, 80:96], ne[:, 96:112], ALU.mult, 16, ("q", "x1"), ("val1",))
+        tt(val[:, 32:48], ne[:, 80:96], ne[:, 112:128], ALU.mult, 16, ("q", "x2"), ("val2",))
+        tt(dd[:, 32:48], ff[:, 0:16], pp[:, 32:48], ALU.subtract, 16, ("f0", "pp"), ("d2",))
+        cp(ff[:, 32:48], pp[:, 32:48], 16, ("pp",), ("f2",))
+        tt(dd[:, 32:48], dd[:, 32:48], ne[:, 48:64], ALU.mult, 16, ("d2", "ne1"), ("d2",))
+        tt(ff[:, 0:16], dd[:, 32:48], pp[:, 32:48], ALU.add, 16, ("d2", "pp"), ("f0",))
+        cp(T.fi[:], ff[:], 48, ("f0", "f1", "f2"), ("fi",))
+        ts(T.uk[:, 0:48], T.fi[:], 4, None, SHR, None, 48, ("fi",), ("uk0",))
+        ts(T.uk[:, 48:96], T.fi[:], 15, None, AND, None, 48, ("fi",), ("uk1",))
+        ul, ud, dl = T["ul%d" % i], T["ud%d" % i], T["dl%d" % i]
+        cp(ul[:], T.uk[:], 96, ("uk0", "uk1"), (("ul", i),))
+        tt(ud[:], T.uk[:, 0:48], T.dm[:, 48:96], ALU.subtract, 48, ("uk0", "dm1"), (("ud", i),))
+        tt(ud[:], ud[:], val[:], ALU.mult, 48, (("ud", i), "val0", "val1", "val2"), (("ud", i),))
+        for p in range(3):
+            add("S", lambda p=p: sca.activation(dl[:, 256 * p:256 * p + 256], T.dtab[:, 0:16].indirect(ul[:, 48 + 16 * p:64 + 16 * p]), ACT.Copy),
+                10.0 + _ga(256), ("dtab", ("ul", i)), (("dl", i, p),))
+
+    def reinforce(i):
+        slot[0] = 6 * i + RS
+        j0 = i - 1
+        ul, ud, dl = T["ul%d" % j0], T["ud%d" % j0], T["dl%d" % j0]
+        tt(T.ww[:], T["bt%d" % i][:], T["d3%d" % j0][:], ALU.is_lt, 48, [("bt", i, 0), ("bt", i, 1)] + [("d3", j0, p) for p in range(3)], ("ww",))
+        tt(T.ww[:], T.ww[:], ud[:], ALU.mult, 48, (("ud", j0), "ww"), ("ww",))
+        tt(T.oc[:, 0:48], T.ww[:], T.dm[:, 0:48], ALU.add, 48, ("ww", "dm0"), ("oc0",))
+        ts(T.oc[:, 48:72], T.ww[:, 1::2], DUO, None, ALU.add, None, 24, ("ww", "duo"), ("oc1",))
+        tt(T.on[:, 0:48], T.dm[:, 96:144], T.ww[:], ALU.subtract, 48, ("ww", "dm2"), ("on0",))
+        ts(T.on[:, 48:72], T.ww[:, 0::2], DUC, -1.0, ALU.add, ALU.mult, 24, ("ww", "duc"), ("on1",))
+        parts = (("phop", 128, 0, 5), ("pe0", 0, 5, 11), ("pe1", 0, 11, 16))
+        for (bk, o, ja, jb) in parts:
+            lst = []
+            for j in range(ja, jb):
+                out = T[bk][:, o + 72 * (j - ja):o + 72 * (j - ja + 1)]
+                lst += [(out, T.seld[:, 128 * j:128 * j + 128], T.oc[:], True, False), (out, T.ih[:], T.on[:], False, True)]
+            mm(lst, ["oc0", "oc1", "on0", "on1", "ih"] + [("seld", j) for j in range(ja, jb)], (bk,))
+        for (bk, o, ja, jb) in parts:
+            ts(T.eq[:, 72 * ja:72 * jb], T[bk][:, o:o + 72 * (jb - ja)], 0.0, None, ALU.is_equal, None, 72 * (jb - ja), (), (("eq", bk),), x=(bk,))
+        cnt = T.phop[:, 64:112]
+        mm([(cnt, T.ih[:], T.oc[:, 0:48], True, False)], ("ih", "oc0"), ("phop",))
+        for (bk, o, ja, jb) in parts:
+            lst = []
+            for j in range(ja, jb):
+                lst += [(T.phop[:, 65:112:2], T.b0[:, 16 - j:144 - j], T.eq[:, 72 * j + 48:72 * j + 72], False, False),
+                        (cnt, T.lall[:, 128 * j:128 * j + 128], T.eq[:, 72 * j:72 * j + 48], False, j == 15)]
+            mm(lst, [("eq", bk), "b0"] + [("lall", j) for j in range(ja, jb)], ("phop",))
+        ts(T.off[:, 0::2], T.phop[:, 64:112:2], DUC, CEN, ALU.min, ALU.add, 24, ("duc",), ("off0",), x=("phop",))
+        ts(T.off[:, 1::2], T.phop[:, 65:112:2], DUO, CEN, ALU.min, ALU.add, 24, ("duo",), ("off1",), x=("phop",))
+        for p in range(3):
+            add("V", lambda p=p: vec.tensor_tensor(T.new[:], T.ph[:, 0:V].indirect(ul[:, 16 * p:16 * p + 16]), dl[:, 256 * p:256 * p + 256], ALU.add),
+                _ga(256), ["ph", ("ul", j0), ("dl", j0, p)] + phi, ("new",))
+            ts(T.new[:], T.new[:], 0.0, 20.0, ALU.max, ALU.min, 256, ("new",), ("new",), 0.5)
+            for h in range(14, -2, -2):
+                add("V", lambda p=p, h=h: vec.tensor_copy(T.ph[:, 0:V + 32].indirect(T.off[:, 16 * p + h:16 * p + h + 2]),
+                                                          T.new[:, 16 * h:16 * h + 32]),
+                    60.0 + 32 * SCT * CY, ("off0", "off1", "new"), ("ph",))
+
+    for i in range(VIS):
+        for s in range(ST):
+            for b in range(2):
+                step(i, s, b)
+        if i >= 1:
+            reinforce(i)
+        if i < VIS - 1:
+            trails(i)
+    cp(T.yvs[:], T["vl%d" % (VIS - 1)][:, 48:64], 16, (("vl", VIS - 1, 3, 0), ("vl", VIS - 1, 3, 1)), ("yvs",))
+    add("S", lambda: sca.dma_start(T.yv[:], T.yvs[:]), 100.0, ("yvs",), (), sem=("o_v", 16), lat=2000.0)
+    add("Y", lambda: g.sync.dma_start(T.yp[:], T.ph[:, 0:V]), 100.0, ("ph",), (), sem=("o_p", 16), lat=4000.0)
+    return ops, nsent[0]
+
+
+def _place(ops, prio, pre):
+    n = len(ops)
+    st = [0.0] * n
+    left = [len(p) for p in pre[0]]
+    busy = {}
+    heap = sorted((prio[k], k) for k in range(n) if not left[k])
+    end = 0.0
+    while heap:
+        k = heap.pop(0)[1]
+        t = pre[2][k]
+        for d, lag in pre[0][k]:
+            if st[d] + lag > t:
+                t = st[d] + lag
+        e, c = ops[k]["eng"], ops[k]["cost"]
+        if e is not None:
+            iv = busy.setdefault(e, [])
+            j = len(iv)
+            while j and iv[j - 1][1] > t:
+                j -= 1
+            while j < len(iv) and iv[j][0] < t + c:
+                t = max(t, iv[j][1])
+                j += 1
+            iv.insert(j, (t, t + c))
+        st[k] = t
+        end = max(end, t + c + pre[3][k])
+        for s in pre[1][k]:
+            left[s] -= 1
+            if not left[s]:
+                it = (prio[s], s)
+                lo, hi = 0, len(heap)
+                while lo < hi:
+                    m = (lo + hi) // 2
+                    if heap[m] < it:
+                        lo = m + 1
+                    else:
+                        hi = m
+                heap.insert(lo, it)
+    return st, end
+
+
+SEED, ROUNDS, JIT, SHAKES, WIN, JIT2 = 1, 100, 500.0, 9000, 2500.0, 500.0
+
+
+def _schedule(ops):
+    n = len(ops)
+    fw = ([[] for _ in ops], [[] for _ in ops], [0.0] * n, [o["lat"] for o in ops])
+    bw = ([[] for _ in ops], [[] for _ in ops], [o["lat"] for o in ops], [0.0] * n)
+    for k, o in enumerate(ops):
+        for d, need in o["deps"].items():
+            lag = ops[d]["lat"] + (HOP if need and o["eng"] is not None else 0.0)
+            fw[0][k].append((d, ops[d]["cost"] + lag))
+            fw[1][d].append(k)
+            bw[0][d].append((k, o["cost"] + lag))
+            bw[1][k].append(d)
+    rng = np.random.default_rng(SEED)
+
+    def back(st, z):
+        rs, _ = _place(ops, [-(st[k] + ops[k]["cost"] + z[k]) for k in range(n)], bw)
+        return [-(rs[k] + ops[k]["cost"]) for k in range(n)]
+    best = None
+    prio = [o["slot"] * 3200.0 + 0.001 * k for k, o in enumerate(ops)]
+    for it in range(ROUNDS):
+        st, end = _place(ops, prio, fw)
+        if best is None or end < best[1]:
+            best = (st, end)
+        prio = back(best[0] if it % 4 == 3 else st, (rng.random(n) * (JIT if it % 2 else 0.0)).tolist())
+    st, end = best
+    cur = np.array(st)
+    for it in range(SHAKES):
+        m = np.abs(cur - rng.random() * end) < WIN * (0.3 + rng.random())
+        s2, e2 = _place(ops, (cur + m * rng.normal(0.0, 1.0, n) * (JIT2 * (0.2 + rng.random()))).tolist(), fw)
+        if it % 8 == 7:
+            s2, e2 = _place(ops, back(s2, [0.0] * n), fw)
+        if e2 <= end:
+            cur, end, st = np.array(s2), e2, s2
+    return sorted(range(n), key=lambda k: (st[k], k)), st, end
+
+
+_ORDER = {}
+
+
+def rank_program(g, core, T, topo):
+    rank = T.rank_of(core)
+    if rank is None:
+        return
+    ops, nsent = _build(g, T, topo, core, rank)
+    if "o" not in _ORDER:
+        _ORDER["o"] = _schedule(ops)
+    queue = {"V": g.vector, "S": g.scalar, "P": g.tensor, "G": g, "Y": g.sync}
+    waited_on = set(d for o in ops if o["eng"] is not None for d, need in o["deps"].items() if need)
+    count = {"V": 0, "S": 0, "P": 0, "G": 0}
+    signal, total = {}, {}
+    seen = {e: {} for e in queue}
+    for k in _ORDER["o"][0]:
+        o = ops[k]
+        e = o["eng"]
+        if e is None:
+            signal[k] = o["sem"]
+            total[o["sem"][0]] = o["sem"][1]
+            continue
+        want = {}
+        for d, need in o["deps"].items():
+            if need:
+                nm, val = signal[d]
+                want[nm] = max(want.get(nm, 0), val)
+        for nm, val in want.items():
+            if seen[e].get(nm, 0) < val:
+                queue[e].wait_ge(T.sem[nm], val)
+                seen[e][nm] = val
+        ins = o["fn"]()
+        if o["sem"] is not None:
+            ins.then_inc(T.sem[o["sem"][0]], o["sem"][1])
+            signal[k] = o["sem"]
+            total[o["sem"][0]] = o["sem"][1]
+        elif k in waited_on:
+            count[e] += 1
+            ins.then_inc(T.sem["c" + e], 1)
+            signal[k] = ("c" + e, count[e])
+            total["c" + e] = count[e]
+    total["sent"] = nsent
+    for nm, val in total.items():
+        if seen["G"].get(nm, 0) < val:
+            g.wait_ge(T.sem[nm], val)

@@ -13,11 +13,11 @@ _SB = {
     "adjs": (V, I32), "xs": (V, BF), "ph": (V + 32, BF), "v0s": (16, I32), "zs": (A, BF), "nzs": (A, BF), "nzk": (A + 16, F16),
     "rr": (256, F32), "rm": (256, F32), "rg": (128, F32), "rq": (40, F32), "pi": (8, I32), "pf": (16, F32),
     "ib": (128, BF), "ih": (128, F16), "i65": (256, BF), "i16": (128, BF), "i4k": (256, F16), "c1": (16, BF), "c2": (16, BF),
-    "rst": (256, F32), "sel": (240, F16), "xm": (128, F16), "b0": (144, BF), "jc": (16, F32), "lc": (16, F32),
+    "rst": (256, F32), "sel": (48, F16), "xm": (128, F16), "b0": (144, BF), "jc": (16, F32), "lc": (16, F32),
     "seld": (2048, F16), "lall": (2048, BF), "dtab": (16, BF), "elf": (40, F32), "el": (40, U16), "dm": (144, F32),
     "wn": (48, I32), "w2": (72, I32), "ki": (64, I32), "k2": (32, I32), "ek": (384, F16),
     "n16": (64, F32), "pp": (48, F32), "ne": (128, F32), "dd": (48, F32), "ff": (48, F32), "fi": (48, I32), "uk": (96, I32),
-    "val": (48, F32), "ww": (48, F32), "oc": (72, F16), "on": (72, F16), "eq": (1152, BF), "off": (48, U16),
+    "val": (48, F32), "ww": (48, F32), "oc": (72, F16), "on": (72, F16), "eq": (576, BF), "off": (48, U16),
     "new": (256, BF), "yvs": (16, F32),
 }
 for _i in range(VIS):
@@ -37,7 +37,7 @@ SEMAPHORES = (["cV", "cS", "cP", "cG", "sent", "l_adj", "l_x", "l_v", "l_z", "l_
               + ["r_z%d" % i for i in (1, 2, 3)]
               + ["r_%s%d%d" % (k, i, b) for k in "vf" for i in (1, 2, 3) for b in (0, 1)])
 
-CY, GA, SCT, PC, HOP = 1.0, 1.56, 3.8, 0.5, 90.0
+CY, GA, SCT, PC, HOP = 1.1, 1.72, 4.5, 0.71, 90.0
 NS, RS, TS = 2.0, 5.5, 8.5
 
 
@@ -94,7 +94,7 @@ def _build(g, T, topo, core, rank):
             for (o, l, rh, st, sp) in lst:
                 ins = pe.matmul(o, l, rh, st, sp)
             return ins
-        return add("P", fn, sum(max(64, q[0].shape[-1]) for q in lst) * PC, r, (), x)
+        return add("P", fn, sum(max(min(64, q[0].shape[0]), q[0].shape[-1]) for q in lst) * PC, r, (), x)
 
     def dst(c):
         rid, pid, _ = topo.addr(c)
@@ -115,17 +115,18 @@ def _build(g, T, topo, core, rank):
         n = add("G", fn, 300.0, r, (), after=after)
         for (c, s, d, es, sem, w) in trs:
             add(None, None, 0.0, (), w, sem=(sem, len(es) * len(d)), lat=lat, after=(n,))
+        last_w["sends"] = len(ops) - 1
 
     def load(q, eng, out, in_, name, sem, lat):
-        return add(eng, lambda: q.dma_start(out, in_), 100.0, (), (name,), sem=(sem, 16), lat=lat)
-    load(g.sync, "Y", T.zs[:], T.z[:], "zs", "l_z", 2500.0)
-    load(sca, "S", T.v0s[:], T.v0[:], "v0s", "l_v", 2500.0)
-    la = load(g.sync, "Y", T.adjs[:], T.adj[:], "adjs", "l_adj", 8000.0)
-    load(sca, "S", T.nzs[:], T.nz[:], "nzs", "l_nz", 3000.0)
-    lx = load(sca, "S", T.xs[:], T.x[:], "xs", "l_x", 8000.0)
+        return add(eng, lambda: q.dma_start(out, in_), 100.0, (), (name,), ("queue" + eng,), sem=(sem, 16), lat=lat)
+    load(g.sync, "Y", T.zs[:], T.z[:], "zs", "l_z", 2200.0)
+    load(sca, "S", T.v0s[:], T.v0[:], "v0s", "l_v", 2200.0)
+    load(sca, "S", T.nzs[:], T.nz[:], "nzs", "l_nz", 2400.0)
+    la = load(g.sync, "Y", T.adjs[:], T.adj[:], "adjs", "l_adj", 7000.0)
+    lx = load(sca, "S", T.xs[:], T.x[:], "xs", "l_x", 7000.0)
 
-    def iota(out, pat, name, n):
-        add("G", lambda: g.iota(out, pat, 0, 0, allow_small_or_imprecise_dtypes=True), 130.0 + 2 * n, (), (name,))
+    def iota(out, pat, name, n, base=0):
+        add("G", lambda: g.iota(out, pat, base, 0, allow_small_or_imprecise_dtypes=True), 130.0 + 2 * n, (), (name,))
     add("G", lambda: g.iota(T.pi[:, 0:1], [[0, 1]], 0, 1), 130.0, (), ("pi0",))
     iota(T.rr[:], [[1, 256]], "rr", 256)
     iota(T.rm[:], [[0, 16], [1, 16]], "rm", 256)
@@ -151,7 +152,7 @@ def _build(g, T, topo, core, rank):
     ts(T.c1[:], T.rq[:, 24:40], PG, -2.0 * SC1, ALU.is_equal, ALU.mult, 16, ("rq1", "pf"), ("c1",))
     ts(T.c2[:], T.rq[:, 24:40], PG, SC1, ALU.is_equal, ALU.mult, 16, ("rq1", "pf"), ("c2",))
     ts(T.rst[:], T.rm[:], 0.0, -67108864.0, ALU.is_equal, ALU.mult, 256, ("rm",), ("rst",))
-    ts(T.sel[:], T.rr[:, 0:240], PM, 112.0, ALU.subtract, ALU.is_equal, 240, ("rr", "pf"), ("sel",))
+    ts(T.sel[:], T.rr[:, 0:48], PM, 16.0, ALU.subtract, ALU.is_equal, 48, ("rr", "pf"), ("sel",))
     ts(T.nzk[:, 0:A], T.nzs[:], 16.0, KK, ALU.mult, ALU.add, A, ("nzs", "kk"), ("nzk0",), 0.5)
     ts(T.nzk[:, A:A + 16], T.nzs[:, 0:16], 16.0, KK, ALU.mult, ALU.add, 16, ("nzs", "kk"), ("nzk1",))
     ts(T.elf[:, 0:4], T.rr[:, 0:8:2], HB1, COND, ALU.add, ALU.mult, 4, ("rr", "hb1", "cond"), ("elf0",))
@@ -170,13 +171,15 @@ def _build(g, T, topo, core, rank):
             ts(T.zr0[:, k::16], T.zs[:], -1.0, None, ALU.mult, None, A, ("zs",), (("zr", 0, k),), 0.5)
     zall = {i: [("zr", i, 0)] for i in range(1, VIS)}
     zall[0] = [("zr", 0, k) for k in range(16)]
-    for i in range(1, VIS):
+
+    def wishes(i, after):
         c = T.cores[(rank + i) % len(T.cores)]
-        send([(c, T.zr0[:], [T["zr%d" % i][:]], topo.engines(core, c), "r_z%d" % i, zall[i])], zall[0], 5000.0 * i, after=(la, lx))
+        send([(c, T.zr0[:], [T["zr%d" % i][:]], topo.engines(core, c), "r_z%d" % i, zall[i])], zall[0], 8000.0, after=after)
+    wishes(1, (la, lx))
     slot[0] = 6.5
     phi = [("phi", q) for q in range(4)]
     for q in range(4):
-        add("V", lambda q=q: vec.memset(T.ph[:, 776 * q:776 * q + 776], 8.0), _v(776, 0.5), (), (("phi", q),))
+        iota(T.ph[:, 776 * q:776 * q + 776], [[0, 776]], ("phi", q), 776, 8)
     iota(T.dm[:, 0:48], [[0, 24], [16, 2]], "dm0", 48)
     ts(T.dm[:, 48:96], T.dm[:, 0:48], DUM, None, ALU.add, None, 48, ("dm0", "dum"), ("dm1",))
     ts(T.dm[:, 96:144], T.dm[:, 0:48], DUC, -1.0, ALU.add, ALU.mult, 48, ("dm0", "duc"), ("dm2",))
@@ -193,8 +196,8 @@ def _build(g, T, topo, core, rank):
     ts(T.dtab[:], T.dtab[:], -3.0, None, ALU.add, None, 16, ("dtab",), ("dtab",))
 
     def hop(out, e, nq, r, bank):
-        mm([(out, T.sel[:, 112 - 16 * c:240 - 16 * c], e[:, 8 * nq * c:8 * nq * (c + 1)], c == 0, c == 7) for c in range(8)],
-           tuple(r) + ("sel",), (bank,))
+        mm([(T[bank][32 * (c // 2):32 * (c // 2) + 32, out:out + 8 * nq], T.sel[:, 16 - 16 * (c % 2):48 - 16 * (c % 2)],
+             e[:, 8 * nq * c:8 * nq * (c + 1)], c % 2 == 0, c % 2 == 1) for c in range(8)], tuple(r) + ("sel",), (bank,))
 
     pcount = [0]
 
@@ -209,9 +212,9 @@ def _build(g, T, topo, core, rank):
         lst = vl[:, 16 * s + 8 * b:16 * s + 8 * b + 8]
         vn = ("vl", i, s, b)
         nzl = T.nzk[:, 128 * b + t:128 * b + t + 128]
-        slot[0] = 2 * t + b - NS
+        slot[0] = 2 * t + 1 - b - NS
         cp(nm[:], T.adjs[:, 0:V].indirect(lst), 128, ("adjs", vn), (("nm", b),), cost=_ga(128))
-        slot[0] = 2 * t + b
+        slot[0] = 2 * t + 1 - b
         ts(nf[:], nm[:], CEN, None, ALU.subtract, None, 128, (("nm", b),), (("nf", b),), 0.5)
         mm([(pk[:, 0:W], nzl, T.i4k[:, 0:W], True, False)], ("nzk0", "nzk1", "i4k0", "i4k1"), (bank,))
         a1n, a2n = [], []
@@ -268,7 +271,7 @@ def _build(g, T, topo, core, rank):
         el = T.el[:, 4:12] if last else T.el[:, 0:4]
         add("V", lambda: vec.tensor_scalar(e1[:, 0:64 * nq], T.wn[:, wn:wn + 24].indirect(el), CEN, None, ALU.subtract),
             _ga(64 * nq), ("wn%d" % b, "wd%d" % b, "el0"), (("e1", b),))
-        hop(pk[:, 256:256 + 8 * nq], e1, nq, (("e1", b),), bank)
+        hop(256, e1, nq, (("e1", b),), bank)
         o = 16 * (s + 1) + 8 * b
         if last:
             dn = T["dn%d" % i][:, 8 * b:8 * b + 8]
@@ -283,7 +286,7 @@ def _build(g, T, topo, core, rank):
                 trs.append((nxt, vl[:, o:o + 8], [T["vl%d" % (i + 1)][:, 8 * b:8 * b + 8]], e_n, "r_v%d%d" % (i + 1, b), (("vl", i + 1, 0, b),)))
                 rd.append(("vl", i, s + 1, b))
             if i > 0:
-                trs.append((prv, dn, [T["bt%d" % i][:, 16 * p + 8 * b:16 * p + 8 * b + 8] for p in range(3)], e_p,
+                trs.append((prv, dn, [T["bt%d" % i][:, 24 * b + 8 * p:24 * b + 8 * p + 8] for p in range(3)], e_p,
                             "r_f%d%d" % (i, b), (("bt", i, b),)))
                 rd.append(("dn", i, b))
             send(trs, rd, 1800.0)
@@ -293,9 +296,12 @@ def _build(g, T, topo, core, rank):
         ts(T.w2[:, 0:64], T.ki[:], 12, 15, SHR, AND, 64, [("ki", s, b) for s in range(3) for b in range(2)], ("w2k",))
         slot[0] = 6 * i + TS
         cp(T.ek[:], T.w2[:, 0:72].indirect(T.el[:, 12:36]), 384, ("w2k", "el1"), ("ek",), cost=_ga(384))
-        hop(T.phop[:, 16:64], T.ek, 6, ("ek",), "phop")
+        hop(16, T.ek, 6, ("ek",), "phop")
         for p in range(3):
-            cp(T["d3%d" % i][:, 16 * p:16 * p + 16], T["dn%d" % i][:], 16, (("dn", i, 0), ("dn", i, 1)), (("d3", i, p),))
+            for b in range(2):
+                add("S", lambda p=p, b=b: sca.activation(T["d3%d" % i][:, 24 * b + 8 * p:24 * b + 8 * p + 8],
+                                                         T["dn%d" % i][:, 8 * b:8 * b + 8], ACT.Copy),
+                    80.0, (("dn", i, b),), (("d3", i, p, b),))
         n16, pp, ne, dd, ff, val = T.n16, T.pp, T.ne, T.dd, T.ff, T.val
         ts(n16[:], T["vl%d" % i][:], 16.0, None, ALU.mult, None, 64, [("vl", i, s, b) for s in range(4) for b in range(2)], ("n16",))
         tt(pp[:], T.phop[:, 16:64], n16[:, 0:48], ALU.add, 48, ("n16",), ("pp",), ("phop",))
@@ -321,8 +327,12 @@ def _build(g, T, topo, core, rank):
         ts(T.uk[:, 48:96], T.fi[:], 15, None, AND, None, 48, ("fi",), ("uk1",))
         ul, ud, dl = T["ul%d" % i], T["ud%d" % i], T["dl%d" % i]
         cp(ul[:], T.uk[:], 96, ("uk0", "uk1"), (("ul", i),))
-        tt(ud[:], T.uk[:, 0:48], T.dm[:, 48:96], ALU.subtract, 48, ("uk0", "dm1"), (("ud", i),))
-        tt(ud[:], ud[:], val[:], ALU.mult, 48, (("ud", i), "val0", "val1", "val2"), (("ud", i),))
+        tt(ff[:], T.uk[:, 0:48], T.dm[:, 48:96], ALU.subtract, 48, ("uk0", "dm1"), ("f0", "f1", "f2"))
+        for p in range(3):
+            for b in range(2):
+                o = 16 * p + 8 * b
+                tt(ud[:, 24 * b + 8 * p:24 * b + 8 * p + 8], ff[:, o:o + 8], val[:, o:o + 8], ALU.mult, 8,
+                   ("f0", "val0", "val1", "val2"), (("ud", i, p, b),))
         for p in range(3):
             add("S", lambda p=p: sca.activation(dl[:, 256 * p:256 * p + 256], T.dtab[:, 0:16].indirect(ul[:, 48 + 16 * p:64 + 16 * p]), ACT.Copy),
                 10.0 + _ga(256), ("dtab", ("ul", i)), (("dl", i, p),))
@@ -331,44 +341,50 @@ def _build(g, T, topo, core, rank):
         slot[0] = 6 * i + RS
         j0 = i - 1
         ul, ud, dl = T["ul%d" % j0], T["ud%d" % j0], T["dl%d" % j0]
-        tt(T.ww[:], T["bt%d" % i][:], T["d3%d" % j0][:], ALU.is_lt, 48, [("bt", i, 0), ("bt", i, 1)] + [("d3", j0, p) for p in range(3)], ("ww",))
-        tt(T.ww[:], T.ww[:], ud[:], ALU.mult, 48, (("ud", j0), "ww"), ("ww",))
-        tt(T.oc[:, 0:48], T.ww[:], T.dm[:, 0:48], ALU.add, 48, ("ww", "dm0"), ("oc0",))
-        ts(T.oc[:, 48:72], T.ww[:, 1::2], DUO, None, ALU.add, None, 24, ("ww", "duo"), ("oc1",))
-        tt(T.on[:, 0:48], T.dm[:, 96:144], T.ww[:], ALU.subtract, 48, ("ww", "dm2"), ("on0",))
-        ts(T.on[:, 48:72], T.ww[:, 0::2], DUC, -1.0, ALU.add, ALU.mult, 24, ("ww", "duc"), ("on1",))
-        parts = (("phop", 128, 0, 5), ("pe0", 0, 5, 11), ("pe1", 0, 11, 16))
-        for (bk, o, ja, jb) in parts:
-            lst = []
-            for j in range(ja, jb):
-                out = T[bk][:, o + 72 * (j - ja):o + 72 * (j - ja + 1)]
-                lst += [(out, T.seld[:, 128 * j:128 * j + 128], T.oc[:], True, False), (out, T.ih[:], T.on[:], False, True)]
-            mm(lst, ["oc0", "oc1", "on0", "on1", "ih"] + [("seld", j) for j in range(ja, jb)], (bk,))
-        for (bk, o, ja, jb) in parts:
-            ts(T.eq[:, 72 * ja:72 * jb], T[bk][:, o:o + 72 * (jb - ja)], 0.0, None, ALU.is_equal, None, 72 * (jb - ja), (), (("eq", bk),), x=(bk,))
-        cnt = T.phop[:, 64:112]
-        mm([(cnt, T.ih[:], T.oc[:, 0:48], True, False)], ("ih", "oc0"), ("phop",))
-        for (bk, o, ja, jb) in parts:
-            lst = []
-            for j in range(ja, jb):
-                lst += [(T.phop[:, 65:112:2], T.b0[:, 16 - j:144 - j], T.eq[:, 72 * j + 48:72 * j + 72], False, False),
-                        (cnt, T.lall[:, 128 * j:128 * j + 128], T.eq[:, 72 * j:72 * j + 48], False, j == 15)]
-            mm(lst, [("eq", bk), "b0"] + [("lall", j) for j in range(ja, jb)], ("phop",))
-        ts(T.off[:, 0::2], T.phop[:, 64:112:2], DUC, CEN, ALU.min, ALU.add, 24, ("duc",), ("off0",), x=("phop",))
-        ts(T.off[:, 1::2], T.phop[:, 65:112:2], DUO, CEN, ALU.min, ALU.add, 24, ("duo",), ("off1",), x=("phop",))
+        for b in (1, 0):
+            o, o3 = 24 * b, 36 * b
+            ww, oc, on = T.ww[:, o:o + 24], T.oc[:, o3:o3 + 36], T.on[:, o3:o3 + 36]
+            tt(ww, T["bt%d" % i][:, o:o + 24], T["d3%d" % j0][:, o:o + 24], ALU.is_lt, 24,
+               [("bt", i, b)] + [("d3", j0, p, b) for p in range(3)], (("ww", b),))
+            tt(ww, ww, ud[:, o:o + 24], ALU.mult, 24, [("ud", j0, p, b) for p in range(3)] + [("ww", b)], (("ww", b),))
+            tt(T.oc[:, o3:o3 + 24], ww, T.dm[:, 0:24], ALU.add, 24, (("ww", b), "dm0"), (("oc0", b),))
+            tt(T.on[:, o3:o3 + 24], T.dm[:, 96:120], ww, ALU.subtract, 24, (("ww", b), "dm2"), (("on0", b),))
+            ts(T.oc[:, o3 + 24:o3 + 36], T.ww[:, o + 1:o + 24:2], DUO, None, ALU.add, None, 12, (("ww", b), "duo"), (("oc1", b),))
+            ts(T.on[:, o3 + 24:o3 + 36], T.ww[:, o:o + 24:2], DUC, -1.0, ALU.add, ALU.mult, 12, (("ww", b), "duc"), (("on1", b),))
+            for q in range(2):
+                bk = "pe%d" % q
+                lst = []
+                for j in range(8):
+                    out = T[bk][:, 36 * j:36 * j + 36]
+                    lst += [(out, T.seld[:, 128 * (8 * q + j):128 * (8 * q + j + 1)], oc, True, False), (out, T.ih[:], on, False, True)]
+                mm(lst, [(n, b) for n in ("oc0", "oc1", "on0", "on1")] + ["ih"] + [("seld", 8 * q + j) for j in range(8)], (bk,))
+            for q in range(2):
+                ts(T.eq[:, 288 * q:288 * q + 288], T["pe%d" % q][:, 0:288], 0.0, None, ALU.is_equal, None, 288, (), (("eq", q),), x=("pe%d" % q,))
+            cnt = T.phop[:, 64:88]
+            mm([(cnt, T.ih[:], T.oc[:, o3:o3 + 24], True, False)], ("ih", ("oc0", b)), ("phop",))
+            for q in range(2):
+                lst = []
+                for j in range(8 * q, 8 * q + 8):
+                    lst += [(T.phop[:, 65:88:2], T.b0[:, 16 - j:144 - j], T.eq[:, 36 * j + 24:36 * j + 36], False, False),
+                            (cnt, T.lall[:, 128 * j:128 * j + 128], T.eq[:, 36 * j:36 * j + 24], False, j == 15)]
+                mm(lst, [("eq", q), "b0"] + [("lall", j) for j in range(8 * q, 8 * q + 8)], ("phop",))
+            ts(T.off[:, o:o + 24:2], T.phop[:, 64:88:2], DUC, CEN, ALU.min, ALU.add, 12, ("duc",), (("off0", b),), x=("phop",))
+            ts(T.off[:, o + 1:o + 24:2], T.phop[:, 65:88:2], DUO, CEN, ALU.min, ALU.add, 12, ("duo",), (("off1", b),), x=("phop",))
         for p in range(3):
             add("V", lambda p=p: vec.tensor_tensor(T.new[:], T.ph[:, 0:V].indirect(ul[:, 16 * p:16 * p + 16]), dl[:, 256 * p:256 * p + 256], ALU.add),
                 _ga(256), ["ph", ("ul", j0), ("dl", j0, p)] + phi, ("new",))
             ts(T.new[:], T.new[:], 0.0, 20.0, ALU.max, ALU.min, 256, ("new",), ("new",), 0.5)
             for h in range(14, -2, -2):
-                add("V", lambda p=p, h=h: vec.tensor_copy(T.ph[:, 0:V + 32].indirect(T.off[:, 16 * p + h:16 * p + h + 2]),
-                                                          T.new[:, 16 * h:16 * h + 32]),
-                    60.0 + 32 * SCT * CY, ("off0", "off1", "new"), ("ph",))
+                c = 24 * (h // 8) + 8 * p + h % 8
+                add("V", lambda c=c, h=h: vec.tensor_copy(T.ph[:, 0:V + 32].indirect(T.off[:, c:c + 2]), T.new[:, 16 * h:16 * h + 32]),
+                    60.0 + 32 * SCT * CY, (("off0", h // 8), ("off1", h // 8), "new"), ("ph",))
 
     for i in range(VIS):
         for s in range(ST):
-            for b in range(2):
+            for b in (1, 0):
                 step(i, s, b)
+        if i + 2 < VIS:
+            wishes(i + 2, (last_w["sends"],))
         if i >= 1:
             reinforce(i)
         if i < VIS - 1:
@@ -419,7 +435,7 @@ def _place(ops, prio, pre):
     return st, end
 
 
-SEED, ROUNDS, JIT, SHAKES, WIN, JIT2 = 1, 100, 500.0, 9000, 2500.0, 500.0
+SEED, ROUNDS, JIT, SHAKES, WIN, JIT2 = 1, 60, 500.0, 13000, 2500.0, 500.0
 
 
 def _schedule(ops):
@@ -428,7 +444,7 @@ def _schedule(ops):
     bw = ([[] for _ in ops], [[] for _ in ops], [o["lat"] for o in ops], [0.0] * n)
     for k, o in enumerate(ops):
         for d, need in o["deps"].items():
-            lag = ops[d]["lat"] + (HOP if need and o["eng"] is not None else 0.0)
+            lag = (ops[d]["lat"] + (HOP if o["eng"] is not None else 0.0)) if need else 0.0
             fw[0][k].append((d, ops[d]["cost"] + lag))
             fw[1][d].append(k)
             bw[0][d].append((k, o["cost"] + lag))
@@ -439,7 +455,7 @@ def _schedule(ops):
         rs, _ = _place(ops, [-(st[k] + ops[k]["cost"] + z[k]) for k in range(n)], bw)
         return [-(rs[k] + ops[k]["cost"]) for k in range(n)]
     best = None
-    prio = [o["slot"] * 3200.0 + 0.001 * k for k, o in enumerate(ops)]
+    prio = [o["slot"] * 3500.0 + 0.001 * k for k, o in enumerate(ops)]
     for it in range(ROUNDS):
         st, end = _place(ops, prio, fw)
         if best is None or end < best[1]:

@@ -5,48 +5,48 @@ from concourse.mybir import AluOpType as ALU, ActivationFunctionType as ACT
 V, A, VIS, ST = 3072, 256, 4, 3
 CEN = 1536.0
 SC1 = 65536.0
+BIG = 4096.0
+NONE = V - CEN + 32
 NV = [[64, 64, 64], [64, 64, 64], [16, 64, 64], [16, 64, 64]]
-VPIECE, SPIECE = 32, 32
+SPIECES = 2
+NOFF = (16, 96, 48, 72)
 F32, BF, F16, I32, U16 = "float32", "bfloat16", "float16", "int32", "uint16"
 
 _SB = {
-    "adjs": (V, I32), "xs": (V, BF), "ph": (V + 32, BF), "v0s": (16, I32), "zs": (A, BF), "nzs": (A, BF), "nzk": (A + 16, F16),
-    "rr": (256, F32), "rm": (256, F32), "rg": (128, F32), "rq": (40, F32), "pi": (8, I32), "pf": (16, F32),
-    "ib": (128, BF), "ih": (128, F16), "i65": (256, BF), "i16": (128, BF), "i4k": (256, F16), "c1": (16, BF), "c2": (16, BF),
-    "rst": (256, F32), "sel": (48, F16), "xm": (128, F16), "b0": (144, BF), "jc": (16, F32), "lc": (16, F32),
-    "seld": (2048, F16), "lall": (2048, BF), "dtab": (16, BF), "elf": (40, F32), "el": (40, U16), "dm": (144, F32),
-    "wn": (48, I32), "w2": (72, I32), "ki": (64, I32), "k2": (32, I32), "ek": (384, F16),
-    "n16": (64, F32), "pp": (48, F32), "ne": (128, F32), "dd": (48, F32), "ff": (48, F32), "fi": (48, I32), "uk": (96, I32),
-    "val": (48, F32), "ww": (48, F32), "oc": (72, F16), "on": (72, F16), "eq": (576, BF), "off": (48, U16),
-    "new": (256, BF), "yvs": (16, F32),
+    "adjs": (V, I32), "xs": (V + 48, BF), "ph": (V + 48, BF), "v0s": (16, I32), "zs": (A, BF), "nzs": (A, BF), "nzk": (A + 16, F16),
+    "rb": (144, BF), "rm": (256, F32), "rq": (48, F32), "pi": (8, I32), "pf": (16, F32), "tg": (48, F32),
+    "zero": (128, BF), "ib": (128, BF), "i4k": (256, BF), "i65": (256, BF), "i2": (128, BF), "i32": (128, BF), "im1": (128, BF),
+    "im64": (128, BF), "im4k": (128, BF), "c1": (16, BF), "c2": (16, BF), "rst": (256, BF), "sel": (48, BF), "b0": (144, BF),
+    "seld": (2048, BF), "rot": (1024, BF), "los": (1024, BF), "ct": (288, BF), "rst2": (288, BF),
+    "elf": (40, F32), "el": (40, U16), "sc": (1024, I32), "wn": (48, I32), "w2": (72, I32), "k2": (16, I32), "ek": (384, F16),
+    "e": (96, BF), "off": (48, U16), "new": (256, BF), "yvs": (16, F32),
 }
 for _i in range(VIS):
-    _SB.update({"zr%d" % _i: (16 * A, BF), "vl%d" % _i: (64, U16), "dn%d" % _i: (16, BF)})
+    _SB.update({"zr%d" % _i: (16 * A, BF), "vl%d" % _i: (112, U16), "nc%d" % _i: (112, F16)})
     if _i > 0:
-        _SB["bt%d" % _i] = (48, BF)
+        _SB.update({"fo%d" % _i: (48, BF), "fb%d" % _i: (48, BF)})
     if _i < VIS - 1:
-        _SB.update({"ul%d" % _i: (96, U16), "d3%d" % _i: (48, BF), "ud%d" % _i: (48, F32), "dl%d" % _i: (768, BF)})
+        _SB.update({"so%d" % _i: (296, F16), "ul%d" % _i: (96, U16), "dl%d" % _i: (768, BF)})
 for _b in range(2):
     _SB.update({"nm%d" % _b: (128, U16), "nf%d" % _b: (128, F16), "pg%d" % _b: (128, BF), "a1%d" % _b: (2048, BF),
-                "a2%d" % _b: (2048, BF), "sc%d" % _b: (256, F32), "e1%d" % _b: (128, F16)})
+                "a2%d" % _b: (2048, BF), "e1%d" % _b: (128, F16), "eq%d" % _b: (384, BF)})
 SCRATCH = {_n: ("sbuf", [128, _w], _d) for _n, (_w, _d) in _SB.items()}
-for _n in ("pk0", "pk1", "pd0", "pd1", "pd2", "pe0", "pe1", "phop"):
-    SCRATCH[_n] = ("psum", [128, 512], F32)
+for _n, _w in (("pd0", 1024), ("pd1", 1024), ("pk0", 512), ("pk1", 512), ("pe0", 512), ("pe1", 512)):
+    SCRATCH[_n] = ("psum", [128, _w], F32)
 
 SEMAPHORES = (["cV", "cS", "cP", "cG", "sent", "l_adj", "l_x", "l_v", "l_z", "l_nz", "o_p", "o_v"]
               + ["r_z%d" % i for i in (1, 2, 3)]
               + ["r_%s%d%d" % (k, i, b) for k in "vf" for i in (1, 2, 3) for b in (0, 1)])
 
-CY, GA, SCT, PC, HOP = 1.1, 1.72, 4.5, 0.71, 90.0
-NS, RS, TS = 2.0, 5.5, 8.5
+CY, GA, SCT, PC, FIX, OWN, HOP = 0.9, 1.56, 3.8, 0.46, 35.0, 70.0, 140.0
 
 
 def _v(n, c=1.0):
-    return max(64.0, n * c) * CY
+    return max(64.0, n * c) * CY + FIX
 
 
 def _ga(n):
-    return 60.0 + n * GA * CY
+    return 55.0 + FIX + n * GA * CY
 
 
 def _build(g, T, topo, core, rank):
@@ -73,8 +73,7 @@ def _build(g, T, topo, core, rank):
             last_w[k] = n
             readers[k] = []
         deps.pop(n, None)
-        ops.append({"eng": eng, "fn": fn, "cost": cost, "deps": deps, "sem": sem, "lat": lat, "slot": slot[0],
-                    "w": (tuple(w) + tuple(x))[:1]})
+        ops.append({"eng": eng, "fn": fn, "cost": cost, "deps": deps, "sem": sem, "lat": lat, "slot": slot[0]})
         return n
 
     def ts(out, in0, s1, s2, o0, o1, n, r, w, c=1.0, x=()):
@@ -109,12 +108,12 @@ def _build(g, T, topo, core, rank):
         nsent[0] += sum(len(t[3]) for t in trs)
 
         def fn():
-            g.remote_dma_fused([RemoteDMATransfer(dst_ids=[dst(c)] * len(d), dma_engine_mask=bits(es), remote_sem=T.sem[sem],
-                                                  srcs=[s], dsts=d) for (c, s, d, es, sem, w) in trs], local_sem=T.sem.sent)
+            g.remote_dma_fused([RemoteDMATransfer(dst_ids=[dst(c)], dma_engine_mask=bits(es), remote_sem=T.sem[sem],
+                                                  srcs=[s], dsts=[d]) for (c, s, d, es, sem, w) in trs], local_sem=T.sem.sent)
             return None
         n = add("G", fn, 300.0, r, (), after=after)
         for (c, s, d, es, sem, w) in trs:
-            add(None, None, 0.0, (), w, sem=(sem, len(es) * len(d)), lat=lat, after=(n,))
+            add(None, None, 0.0, (), w, sem=(sem, len(es)), lat=lat, after=(n,))
         last_w["sends"] = len(ops) - 1
 
     def load(q, eng, out, in_, name, sem, lat):
@@ -122,51 +121,50 @@ def _build(g, T, topo, core, rank):
     load(g.sync, "Y", T.zs[:], T.z[:], "zs", "l_z", 2200.0)
     load(sca, "S", T.v0s[:], T.v0[:], "v0s", "l_v", 2200.0)
     load(sca, "S", T.nzs[:], T.nz[:], "nzs", "l_nz", 2400.0)
-    la = load(g.sync, "Y", T.adjs[:], T.adj[:], "adjs", "l_adj", 7000.0)
-    lx = load(sca, "S", T.xs[:], T.x[:], "xs", "l_x", 7000.0)
+    la = load(g.sync, "Y", T.adjs[:], T.adj[:], "adjs", "l_adj", 6500.0)
+    lx = load(sca, "S", T.xs[:, 0:V], T.x[:], "xs", "l_x", 8000.0)
 
-    def iota(out, pat, name, n, base=0):
-        add("G", lambda: g.iota(out, pat, base, 0, allow_small_or_imprecise_dtypes=True), 130.0 + 2 * n, (), (name,))
+    def iota(out, pat, name, base=0):
+        add("G", lambda: g.iota(out, pat, base, 0, allow_small_or_imprecise_dtypes=True), 130.0 + 1.8 * out.shape[-1], (), (name,))
+
+    def mark(out, in_, pat, fill, base, r, name):
+        add("G", lambda: g.affine_select(out, in_, pat, ALU.not_equal, fill, base, 1), 170.0 + 1.8 * out.shape[-1], r, (name,))
     add("G", lambda: g.iota(T.pi[:, 0:1], [[0, 1]], 0, 1), 130.0, (), ("pi0",))
-    iota(T.rr[:], [[1, 256]], "rr", 256)
-    iota(T.rm[:], [[0, 16], [1, 16]], "rm", 256)
-    iota(T.rg[:], [[1, 8], [0, 16]], "rg", 128)
-    iota(T.rq[:, 0:24], [[1, 8], [16, 3]], "rq0", 24)
-    iota(T.rq[:, 24:40], [[0, 2], [1, 8]], "rq1", 16)
+    iota(T.rb[:], [[1, 144]], "rb")
+    iota(T.rq[:, 0:24], [[1, 8], [16, 3]], "rq0")
+    iota(T.rq[:, 24:40], [[0, 2], [1, 8]], "rq1")
+    iota(T.rm[:], [[0, 16], [1, 16]], "rm")
     AND, SHR = ALU.bitwise_and, ALU.logical_shift_right
     ts(T.pi[:, 1:2], T.pi[:, 0:1], 15, None, AND, None, 1, ("pi0",), ("pi1",))
     ts(T.pi[:, 2:3], T.pi[:, 0:1], 4, None, SHR, None, 1, ("pi0",), ("pi2",))
     ts(T.pi[:, 3:4], T.pi[:, 0:1], 7, None, AND, None, 1, ("pi0",), ("pi3",))
     ts(T.pi[:, 4:5], T.pi[:, 0:1], 3, 1, SHR, AND, 1, ("pi0",), ("pi4",))
     cp(T.pf[:, 0:5], T.pi[:, 0:5], 5, ("pi0", "pi1", "pi2", "pi3", "pi4"), ("pf",))
-    P, PM, PG, P7, HB, COND, KK, DUM, DUC, HB1, HB8, G16, DUO, HB2 = (T.pf[:, k:k + 1] for k in range(14))
+    P, PM, PG, P7, HB, COND, KK, KH, DUC, DUO, HB1, HB2, HB8, G16 = (T.pf[:, k:k + 1] for k in range(14))
     tt(COND, P7, PG, ALU.is_equal, 1, ("pf",), ("cond",))
-    for (col, src, m, a, name) in ((KK, PM, -1.0, 15.0, "kk"), (DUM, PM, 1.0, float(V), "dum"), (DUC, PM, 1.0, V - CEN, "duc"),
+    for (col, src, m, a, name) in ((KK, PM, -1.0, 15.0, "kk"), (KH, PM, -1.0, 15.5, "kh"), (DUC, PM, 1.0, V - CEN, "duc"),
                                    (DUO, PM, 1.0, V - CEN + 16, "duo"), (HB1, HB, 1.0, -16.0, "hb1"), (HB2, HB, 8.0, -16.0, "hb2"),
                                    (HB8, HB, 8.0, -64.0, "hb8"), (G16, PG, 16.0, 16.0, "g16")):
-        ts(col, src, m, a, ALU.mult, ALU.add, 1, ("pf",), (name,))
-    ts(T.ib[:], T.rr[:, 0:128], P, None, ALU.is_equal, None, 128, ("rr", "pf"), ("ib",))
-    for (out, m, name) in ((T.ih[:], 1.0, "ih"), (T.i4k[:, 0:128], 4096.0, "i4k0"), (T.i4k[:, 128:256], 4096.0, "i4k1"),
-                           (T.i65[:, 0:128], SC1, "i650"), (T.i65[:, 128:256], SC1, "i651"), (T.i16[:], 16.0, "i16")):
+        add("S", lambda col=col, src=src, m=m, a=a: sca.activation(col, src, ACT.Copy, bias=a, scale=m), _v(1), ("pf",), (name,))
+    ts(T.ib[:], T.rb[:, 0:128], P, None, ALU.is_equal, None, 128, ("rb", "pf"), ("ib",), 0.5)
+    for (out, m, name) in ((T.i4k[:, 0:128], BIG, "i4k0"), (T.i4k[:, 128:256], BIG, "i4k1"), (T.i2[:], 2.0, "i2"), (T.im1[:], -1.0, "im1"),
+                           (T.zero[:], 0.0, "zero"), (T.i65[:, 0:128], SC1, "i650"), (T.i65[:, 128:256], SC1, "i651"),
+                           (T.i32[:], 32.0, "i32"), (T.im64[:], -64.0, "im64"), (T.im4k[:], -BIG, "im4k")):
         ts(out, T.ib[:], m, None, ALU.mult, None, 128, ("ib",), (name,), 0.5)
     ts(T.c1[:], T.rq[:, 24:40], PG, -2.0 * SC1, ALU.is_equal, ALU.mult, 16, ("rq1", "pf"), ("c1",))
     ts(T.c2[:], T.rq[:, 24:40], PG, SC1, ALU.is_equal, ALU.mult, 16, ("rq1", "pf"), ("c2",))
     ts(T.rst[:], T.rm[:], 0.0, -67108864.0, ALU.is_equal, ALU.mult, 256, ("rm",), ("rst",))
-    ts(T.sel[:], T.rr[:, 0:48], PM, 16.0, ALU.subtract, ALU.is_equal, 48, ("rr", "pf"), ("sel",))
-    ts(T.nzk[:, 0:A], T.nzs[:], 16.0, KK, ALU.mult, ALU.add, A, ("nzs", "kk"), ("nzk0",), 0.5)
-    ts(T.nzk[:, A:A + 16], T.nzs[:, 0:16], 16.0, KK, ALU.mult, ALU.add, 16, ("nzs", "kk"), ("nzk1",))
-    ts(T.elf[:, 0:4], T.rr[:, 0:8:2], HB1, COND, ALU.add, ALU.mult, 4, ("rr", "hb1", "cond"), ("elf0",))
-    ts(T.elf[:, 4:12], T.rr[:, 0:8], HB2, COND, ALU.add, ALU.mult, 8, ("rr", "hb2", "cond"), ("elf1",))
+    ts(T.sel[:], T.rb[:, 0:48], PM, 16.0, ALU.subtract, ALU.is_equal, 48, ("rb", "pf"), ("sel",))
+    ts(T.nzk[:, 0:A], T.nzs[:], 16.0, KH, ALU.mult, ALU.add, A, ("nzs", "kh"), ("nzk0",), 0.5)
+    ts(T.nzk[:, A:A + 16], T.nzs[:, 0:16], 16.0, KH, ALU.mult, ALU.add, 16, ("nzs", "kh"), ("nzk1",))
+    ts(T.elf[:, 0:4], T.rb[:, 0:8:2], HB1, COND, ALU.add, ALU.mult, 4, ("rb", "hb1", "cond"), ("elf0",))
+    ts(T.elf[:, 4:12], T.rb[:, 0:8], HB2, COND, ALU.add, ALU.mult, 8, ("rb", "hb2", "cond"), ("elf1",))
     ts(T.el[:, 0:12], T.elf[:, 0:12], 16.0, None, ALU.add, None, 12, ("elf0", "elf1"), ("el0",))
-    ts(T.rq[:, 2:24:3], T.rq[:, 2:24:3], HB8, 64.0, ALU.add, ALU.add, 8, ("rq0", "hb8"), ("rq0",))
-    ts(T.elf[:, 12:36], T.rq[:, 0:24], HB8, COND, ALU.add, ALU.mult, 24, ("rq0", "hb8", "cond"), ("elf2",))
-    ts(T.el[:, 12:36], T.elf[:, 12:36], 64.0, None, ALU.add, None, 24, ("elf2",), ("el1",))
     add("V", lambda: vec.memset(T.wn[:], int(CEN)), _v(48), (), ("wn0", "wn1", "wd0", "wd1"))
-    add("V", lambda: vec.memset(T.w2[:], 0), _v(72), (), ("w2k",))
-    cp(T.vl0[:, 0:16], T.v0s[:], 16, ("v0s",), (("vl", 0, 0, 0), ("vl", 0, 0, 1)))
+    cp(T.vl0[:, 16:32], T.v0s[:], 16, ("v0s",), (("vl", 0, 0, 0), ("vl", 0, 0, 1)))
     for k in range(16):
         if k % 2:
-            add("S", lambda k=k: sca.activation(T.zr0[:, k::16], T.zs[:], ACT.Copy, scale=-1.0), 70.0 + A * CY, ("zs",), (("zr", 0, k),))
+            add("S", lambda k=k: sca.activation(T.zr0[:, k::16], T.zs[:], ACT.Copy, scale=-1.0), _v(A), ("zs",), (("zr", 0, k),))
         else:
             ts(T.zr0[:, k::16], T.zs[:], -1.0, None, ALU.mult, None, A, ("zs",), (("zr", 0, k),), 0.5)
     zall = {i: [("zr", i, 0)] for i in range(1, VIS)}
@@ -174,30 +172,47 @@ def _build(g, T, topo, core, rank):
 
     def wishes(i, after):
         c = T.cores[(rank + i) % len(T.cores)]
-        send([(c, T.zr0[:], [T["zr%d" % i][:]], topo.engines(core, c), "r_z%d" % i, zall[i])], zall[0], 8000.0, after=after)
+        send([(c, T.zr0[:], T["zr%d" % i][:], topo.engines(core, c), "r_z%d" % i, zall[i])], zall[0], 6000.0, after=after)
     wishes(1, (la, lx))
-    slot[0] = 6.5
-    phi = [("phi", q) for q in range(4)]
-    for q in range(4):
-        iota(T.ph[:, 776 * q:776 * q + 776], [[0, 776]], ("phi", q), 776, 8)
-    iota(T.dm[:, 0:48], [[0, 24], [16, 2]], "dm0", 48)
-    ts(T.dm[:, 48:96], T.dm[:, 0:48], DUM, None, ALU.add, None, 48, ("dm0", "dum"), ("dm1",))
-    ts(T.dm[:, 96:144], T.dm[:, 0:48], DUC, -1.0, ALU.add, ALU.mult, 48, ("dm0", "duc"), ("dm2",))
-    ts(T.dm[:, 0:48], T.dm[:, 0:48], DUC, None, ALU.add, None, 48, ("dm0", "duc"), ("dm0",))
-    ts(T.jc[:], T.rr[:, 0:16], PM, None, ALU.is_equal, None, 16, ("rr", "pf"), ("jc",))
-    ts(T.lc[:], T.rr[:, 0:16], PM, None, ALU.is_gt, None, 16, ("rr", "pf"), ("lc",))
-    ts(T.xm[:], T.rg[:], PG, None, ALU.is_equal, None, 128, ("rg", "pf"), ("xm",))
-    ts(T.b0[:], T.rr[:, 0:144], G16, 4096.0, ALU.is_equal, ALU.mult, 144, ("rr", "g16"), ("b0",))
+    slot[0] = -1.0
+    ts(T.rq[:, 2:24:3], T.rq[:, 2:24:3], HB8, 64.0, ALU.add, ALU.add, 8, ("rq0", "hb8"), ("rq0",))
+    ts(T.elf[:, 12:36], T.rq[:, 0:24], HB8, COND, ALU.add, ALU.mult, 24, ("rq0", "hb8", "cond"), ("elf2",))
+    ts(T.el[:, 12:36], T.elf[:, 12:36], 64.0, None, ALU.add, None, 24, ("elf2",), ("el1",))
+    add("V", lambda: vec.memset(T.w2[:], 0), _v(72), (), ("w2k",))
+    ts(T.xs[:, V:V + 48], T.rm[:, 0:48], KK, 11.0, ALU.is_equal, ALU.mult, 48, ("rm", "kk"), ("dtab",))
+    ts(T.xs[:, V:V + 48], T.xs[:, V:V + 48], -3.0, None, ALU.add, None, 48, ("dtab",), ("dtab",))
+    sr, tr_, tl = T.rb[:, 1:9], T.tg[:, 0:8], T.tg[:, 8:16]
+    ts(tr_, sr, PM, 16.0, ALU.is_gt, ALU.mult, 8, ("rb", "pf"), ("tr",))
+    tt(tr_, tr_, sr, ALU.subtract, 8, ("tr", "rb"), ("tr",))
+    ts(tr_, tr_, P, None, ALU.add, None, 8, ("tr", "pf"), ("tr",))
+    ts(tl, sr, KK, None, ALU.is_le, None, 8, ("rb", "kk"), ("tl",))
+    tt(tl, tl, sr, ALU.mult, 8, ("tl", "rb"), ("tl",))
+    ts(tl, tl, P, None, ALU.add, None, 8, ("tl", "pf"), ("tl",))
+    for s in range(8):
+        o = 128 * s
+        ts(T.rot[:, o:o + 128], T.rb[:, 0:128], T.tg[:, s:s + 1], None, ALU.is_equal, None, 128, ("rb", "tr"), (("rot", s),), 0.5)
+        mark(T.rot[:, o:o + 128], T.rot[:, o:o + 128], [[-1, 128]], -1.0, 0, (("rot", s),), ("rot", s))
+        ts(T.los[:, o:o + 128], T.rb[:, 0:128], T.tg[:, 8 + s:9 + s], BIG, ALU.is_equal, ALU.mult, 128, ("rb", "tl"), (("los", s),), 0.5)
+    ts(T.b0[:], T.rb[:], G16, BIG, ALU.is_equal, ALU.mult, 144, ("rb", "g16"), ("b0",), 0.5)
+    iota(T.ct[:, 0:144:3], [[-16, 3], [0, 16]], "ct0", 32)
+    iota(T.ct[:, 1:96:3], [[-16, 2], [0, 16]], "ct1", 80)
+    iota(T.ct[:, 2:48:3], [[0, 16]], "ct2", 64)
+    iota(T.ct[:, 97:288:3], [[0, 64]], "ct3", int(BIG))
+    iota(T.ct[:, 50:288:3], [[0, 80]], "ct4", int(BIG))
+    iota(T.ct[:, 144:288:3], [[0, 48]], "ct5", 0)
+    iota(T.rst2[:, 0:288:3], [[0, 96]], "rs0", int(NONE))
+    iota(T.rst2[:, 1:288:3], [[0, 96]], "rs1", -16384)
+    iota(T.rst2[:, 2:288:3], [[0, 96]], "rs2", -16384)
+    slot[0] = 1.0
     for j in range(16):
-        ts(T.seld[:, 128 * j:128 * j + 128], T.xm[:], T.jc[:, j:j + 1], None, ALU.mult, None, 128, ("xm", "jc"), (("seld", j),), 0.5)
-        ts(T.lall[:, 128 * j:128 * j + 128], T.b0[:, 16 - j:144 - j], T.lc[:, j:j + 1], None, ALU.mult, None, 128,
-           ("b0", "lc"), (("lall", j),), 0.5)
-    ts(T.dtab[:], T.rr[:, 0:16], KK, 11.0, ALU.is_equal, ALU.mult, 16, ("rr", "kk"), ("dtab",))
-    ts(T.dtab[:], T.dtab[:], -3.0, None, ALU.add, None, 16, ("dtab",), ("dtab",))
+        mark(T.seld[:, 128 * j:128 * j + 128], T.zero[:], [[-16, 8], [0, 16]], 1.0, -j, ("zero",), ("seld", j))
+    phi = [("phi", q) for q in range(8)]
+    for q in range(8):
+        iota(T.ph[:, 390 * q:390 * q + 390], [[0, 390]], ("phi", q), 8)
 
-    def hop(out, e, nq, r, bank):
-        mm([(T[bank][32 * (c // 2):32 * (c // 2) + 32, out:out + 8 * nq], T.sel[:, 16 - 16 * (c % 2):48 - 16 * (c % 2)],
-             e[:, 8 * nq * c:8 * nq * (c + 1)], c % 2 == 0, c % 2 == 1) for c in range(8)], tuple(r) + ("sel",), (bank,))
+    def hop(bank, out, e, n):
+        return [(T[bank][32 * (c // 2):32 * (c // 2) + 32, out], T.sel[:, 16 - 16 * (c % 2):48 - 16 * (c % 2)], e(c)) + n(c)
+                for c in range(8)]
 
     pcount = [0]
 
@@ -207,179 +222,185 @@ def _build(g, T, topo, core, rank):
         nv = NV[i][s]
         W = 256 if last else 128
         vl, zr = T["vl%d" % i], T["zr%d" % i]
-        nm, nf, pg, a1, a2, sc, e1, pk = (T["%s%d" % (n, b)] for n in ("nm", "nf", "pg", "a1", "a2", "sc", "e1", "pk"))
+        nm, nf, pg, a1, a2, e1, pk = (T["%s%d" % (n, b)] for n in ("nm", "nf", "pg", "a1", "a2", "e1", "pk"))
         bank = "pk%d" % b
-        lst = vl[:, 16 * s + 8 * b:16 * s + 8 * b + 8]
+        lst = vl[:, NOFF[s] + 8 * b:NOFF[s] + 8 * b + 8]
         vn = ("vl", i, s, b)
         nzl = T.nzk[:, 128 * b + t:128 * b + t + 128]
-        slot[0] = 2 * t + 1 - b - NS
+        slot[0] = 2 * t + 1 - b - 2.0
         cp(nm[:], T.adjs[:, 0:V].indirect(lst), 128, ("adjs", vn), (("nm", b),), cost=_ga(128))
         slot[0] = 2 * t + 1 - b
-        ts(nf[:], nm[:], CEN, None, ALU.subtract, None, 128, (("nm", b),), (("nf", b),), 0.5)
+        ts(nf[:], nm[:], 2048.0, None, ALU.subtract, None, 128, (("nm", b),), (("nf", b),), 0.5)
         mm([(pk[:, 0:W], nzl, T.i4k[:, 0:W], True, False)], ("nzk0", "nzk1", "i4k0", "i4k1"), (bank,))
-        a1n, a2n = [], []
-        for c0 in range(nv, 128, SPIECE):
-            c1 = min(128, c0 + SPIECE)
+        a1n = []
+        cuts = [nv + 2 * ((128 - nv) * q // (2 * SPIECES)) for q in range(SPIECES + 1)]
+        for c0, c1 in zip(cuts, cuts[1:]):
             n = 16 * (c1 - c0)
-            pn = "pd%d" % (pcount[0] % 3)
+            pn = "pd%d" % (pcount[0] % 2)
             pcount[0] += 1
             pd = T[pn]
-            n1, n2 = [("a1", b, c) for c in range(c0, c1, 8)], [("a2", b, c) for c in range(c0, c1, 8)]
+            n1, n2 = ("a1", b, pn), ("a2", b, pn)
             add("S", lambda c0=c0, c1=c1: sca.activation(a2[:, 16 * c0:16 * c1], T.xs[:, 0:V].indirect(nm[:, c0:c1]), ACT.Copy),
-                10.0 + _ga(n), ("xs", ("nm", b)), n2)
-            mm([(pd[:, 0:n], T.ib[:], zr[:, 2048 * b + 16 * c0:2048 * b + 16 * c1], True, False)], ["ib"] + zall[i], (pn,))
-            mm([(pd[:, 0:n], T.ib[:], a2[:, 16 * c0:16 * c1], False, True)], ["ib"] + n2, (pn,))
+                10.0 + _ga(n), ("xs", ("nm", b)), (n2, ("a2", b, "v")) if c0 == 0 else (n2,))
+            for o in range(0, n, 512):
+                e = min(n, o + 512)
+                mm([(pd[:, o:e], T.ib[:], zr[:, 2048 * b + 16 * c0 + o:2048 * b + 16 * c0 + e], True, False),
+                    (pd[:, o:e], T.ib[:], a2[:, 16 * c0 + o:16 * c0 + e], False, True)], ["ib", n2] + zall[i], (pn,))
             add("S", lambda c0=c0, c1=c1, pd=pd, n=n: sca.activation(a1[:, 16 * c0:16 * c1], pd[:, 0:n], ACT.Abs, scale=0.5),
-                70.0 + n * CY, (), n1, (pn,))
-            a1n += n1
-        for c0 in range(0, nv, VPIECE):
-            c1 = min(nv, c0 + VPIECE)
-            n = 16 * (c1 - c0)
-            n1, n2 = [("a1", b, c) for c in range(c0, c1, 8)], [("a2", b, c) for c in range(c0, c1, 8)]
-            add("V", lambda c0=c0, c1=c1: vec.tensor_tensor(a2[:, 16 * c0:16 * c1], T.xs[:, 0:V].indirect(nm[:, c0:c1]),
-                                                            zr[:, 2048 * b + 16 * c0:2048 * b + 16 * c1], ALU.add),
-                _ga(n), ["xs", ("nm", b)] + zall[i], n2)
-            ts(a1[:, 16 * c0:16 * c1], a2[:, 16 * c0:16 * c1], 0.0, None, ALU.max, None, n, n2, n1, 0.5)
-            a1n += n1
-            a2n += n2
+                _v(n), (), (n1, ("a1", b, "v")) if c0 == 0 else (n1,), (pn,))
+            a1n.append(n1)
         if nv:
-            mm([(pk[0:nv, k:W:16], a2[:, k:16 * nv:16], T.c2[:, 0:W // 16], False, False) for k in range(16)], a2n + ["c2"], (bank,))
-        mm([(pk[:, k:W:16], a1[:, k:2048:16], T.c1[:, 0:W // 16], False, False) for k in range(16)], a1n + ["c1"], (bank,))
-        fin, rd = [], [("nf", b), "ih", "nzk0", "nzk1"]
+            n = 16 * nv
+            n1, n2 = ("a1", b, "v"), ("a2", b, "v")
+            add("V", lambda: vec.tensor_tensor(a2[:, 0:n], T.xs[:, 0:V].indirect(nm[:, 0:nv]), zr[:, 2048 * b:2048 * b + n], ALU.add),
+                _ga(n), ["xs", ("nm", b)] + zall[i], (n2,))
+            ts(a1[:, 0:n], a2[:, 0:n], 0.0, None, ALU.max, None, n, (n2,), (n1,), 0.5)
+            a1n.append(n1)
+            mm([(pk[0:nv, k:W:16], a2[:, k:16 * nv:16], T.c2[:, 0:W // 16], False, False) for k in range(16)], (n2, "c2"), (bank,))
+        k1, k2 = (128, 0) if last and b == 0 else (0, 128)
         if i >= 2:
             add("S", lambda: sca.activation(pg[:], T.ph[:, 0:V].indirect(lst), ACT.Copy), 10.0 + _ga(128), ("ph", vn), (("pg", b),))
+        allw = [(n, b, q) for n in ("a1", "a2") for q in ("pd0", "pd1", "v")]
+        mm([(pk[:, k:W:16], a1[:, k:2048:16], T.c1[:, 0:W // 16], False, False) for k in range(16)], allw + ["c1"], (bank,))
+        fin, rd = [], [("nf", b), "ib", "i2", "nzk0", "nzk1"]
+        if i >= 2:
             fin.append((pk[:, 0:W], pg[:], T.i65[:, 0:W], False, False))
-            rd += [("pg", b), "i650", "i651", "i16"]
+            rd += [("pg", b), "i650", "i651", "i32"]
             if last:
-                fin.append((pk[:, 128:256], pg[:], T.i16[:], False, False))
+                fin.append((pk[:, k2:k2 + 128], pg[:], T.i32[:], False, False))
         if last:
-            fin.append((pk[:, 128:256], nzl, T.ih[:], False, False))
-        fin.append((pk[:, 0:128], nf[:], T.ih[:], False, True))
+            fin.append((pk[:, k2:k2 + 128], nzl, T.i2[:], False, False))
+        fin.append((pk[:, k1:k1 + 128], nf[:], T.ib[:], False, True))
         mm(fin, rd, (bank,))
-        add("V", lambda: vec.tensor_tensor_scan(sc[:, 0:W], T.rst[:, 0:W], pk[:, 0:W], 0.0, ALU.add, ALU.max), _v(W),
-            ("rst",), (("sc", b),), (bank,))
-        nq = 2 if last else 1
-        ko = 32 + 16 * b if last else 16 * s + 8 * b
+        so = 512 + 256 * b if last else 256 * s + 128 * b
+        sc, scn = T.sc[:, so:so + W], ("sc", s, b)
+        add("V", lambda: vec.tensor_tensor_scan(sc, T.rst[:, 0:W], pk[:, 0:W], 0.0, ALU.add, ALU.max), _v(W), ("rst",), (scn,), (bank,))
+        nq = W // 128
         wn = 24 * b
-        ts(T.ki[:, ko:ko + 8 * nq], sc[:, 15:W:16], CEN, None, ALU.add, None, 8, (("sc", b),), (("ki", s, b),))
-        ts(T.wn[:, wn:wn + 8], T.ki[:, ko:ko + 8], 4095, None, AND, None, 8, (("ki", s, b),), ("wn%d" % b,))
+        ts(T.wn[:, wn:wn + 8 * nq], sc[:, 15:W:16], 4095, None, AND, None, 8, (scn,), ("wn%d" % b, "wd%d" % b))
         if last:
-            k2, ka, kc = T.ki[:, ko + 8:ko + 16], T.k2[:, 16 * b:16 * b + 8], T.k2[:, 16 * b + 8:16 * b + 16]
-            ts(ka, k2, 4095, 4, AND, SHR, 8, (("ki", s, b),), (("k2a", b),))
-            ts(kc, k2, 16, None, ALU.arith_shift_right, None, 8, (("ki", s, b),), (("k2c", b),))
-            tt(T.wn[:, wn + 8:wn + 16], ka, kc, ALU.subtract, 8, (("k2a", b), ("k2c", b)), ("wd%d" % b,))
+            kc, wd = T.k2[:, 8 * b:8 * b + 8], T.wn[:, wn + k2 // 16:wn + k2 // 16 + 8]
+            ts(kc, sc[:, k2 + 15:k2 + 128:16], 11, None, ALU.arith_shift_right, None, 8, (scn,), (("k2", b),))
+            tt(wd, wd, kc, ALU.subtract, 8, (("k2", b), "wd%d" % b), ("wd%d" % b,))
         el = T.el[:, 4:12] if last else T.el[:, 0:4]
         add("V", lambda: vec.tensor_scalar(e1[:, 0:64 * nq], T.wn[:, wn:wn + 24].indirect(el), CEN, None, ALU.subtract),
             _ga(64 * nq), ("wn%d" % b, "wd%d" % b, "el0"), (("e1", b),))
-        hop(256, e1, nq, (("e1", b),), bank)
-        o = 16 * (s + 1) + 8 * b
-        if last:
-            dn = T["dn%d" % i][:, 8 * b:8 * b + 8]
-            ts(dn, pk[:, 264:272], CEN - CEN / 16, None, ALU.add, None, 8, (), (("dn", i, b),), x=(bank,))
-        ts(vl[:, o:o + 8], pk[:, 256:264], CEN, None, ALU.add, None, 8, (), (("vl", i, s + 1, b),), x=(bank,))
+        lst2 = hop(bank, slice(256, 256 + 8 * nq), lambda c: e1[:, 8 * nq * c:8 * nq * (c + 1)], lambda c: (c % 2 == 0, c % 2 == 1))
+        rd = [("e1", b), "sel"]
+        if last and i > 0:
+            dp = T["nc%d" % i][:, 8 + 24 * b:16 + 24 * b]
+            for p in range(3):
+                o = 272 + 8 * p
+                lst2.append((pk[:, o:o + 8], T.im1[:], dp, True, False))
+                lst2 += hop(bank, slice(o, o + 8), lambda c: e1[:, 16 * c + k2 // 16:16 * c + k2 // 16 + 8], lambda c: (False, c % 2 == 1))
+            rd += ["im1", ("nc", i, 0)]
+        mm(lst2, rd, (bank,))
+        o = 64 + 16 * b if last else NOFF[s + 1] + 8 * b
+        if last and i > 0:
+            fo = T["fo%d" % i][:, 24 * b:24 * b + 24]
+            ts(fo, pk[:, 272:296], 0.0, BIG, ALU.is_ge, ALU.mult, 24, (), (("fo", i, b),), x=(bank,))
+        ts(vl[:, o:o + 8 * nq], pk[:, 256:256 + 8 * nq], CEN, None, ALU.add, None, 8, (), (("vl", i, s + 1, b),), x=(bank,))
         if last:
             trs, rd = [], []
             e_n, e_p = topo.engines(core, nxt), topo.engines(core, prv)
             if 0 < i < VIS - 1:
                 e_n, e_p = e_n[:len(e_n) // 2], e_p[len(e_p) // 2:]
             if i < VIS - 1:
-                trs.append((nxt, vl[:, o:o + 8], [T["vl%d" % (i + 1)][:, 8 * b:8 * b + 8]], e_n, "r_v%d%d" % (i + 1, b), (("vl", i + 1, 0, b),)))
-                rd.append(("vl", i, s + 1, b))
+                trs.append((nxt, vl[:, 56 + 24 * b:80 + 24 * b], T["vl%d" % (i + 1)][:, 24 * b:24 * b + 24], e_n,
+                            "r_v%d%d" % (i + 1, b), (("vl", i + 1, 0, b),)))
+                rd += [("vl", i, 3, b), ("vl", i, 2 - b, 1 - b)]
             if i > 0:
-                trs.append((prv, dn, [T["bt%d" % i][:, 24 * b + 8 * p:24 * b + 8 * p + 8] for p in range(3)], e_p,
-                            "r_f%d%d" % (i, b), (("bt", i, b),)))
-                rd.append(("dn", i, b))
+                trs.append((prv, fo, T["fb%d" % i][:, 24 * b:24 * b + 24], e_p, "r_f%d%d" % (i, b), (("fb", i, b),)))
+                rd.append(("fo", i, b))
             send(trs, rd, 1800.0)
 
+    def centre(i, q, lo, hi, r):
+        ts(T["nc%d" % i][:, lo:hi], T["vl%d" % i][:, lo:hi], CEN, None, ALU.subtract, None, hi - lo, r, (("nc", i, q),), 0.5)
+
     def trails(i):
-        slot[0] = 6 * i + 5
-        ts(T.w2[:, 0:64], T.ki[:], 12, 15, SHR, AND, 64, [("ki", s, b) for s in range(3) for b in range(2)], ("w2k",))
-        slot[0] = 6 * i + TS
+        slot[0] = 6 * i + 6.5
+        nc, so, ul, dl, pb = T["nc%d" % i], T["so%d" % i], T["ul%d" % i], T["dl%d" % i], T.pe1
+        ts(T.w2[:, 0:64], T.sc[:, 15:1024:16], 12, 15, SHR, AND, 64, [("sc", s, b) for s in range(3) for b in range(2)], ("w2k",))
+        centre(i, 1, 48, 112, [("vl", i, s, b) for s in (1, 2, 3) for b in range(2)])
+        slot[0] = 6 * i + 8.5
         cp(T.ek[:], T.w2[:, 0:72].indirect(T.el[:, 12:36]), 384, ("w2k", "el1"), ("ek",), cost=_ga(384))
-        hop(16, T.ek, 6, ("ek",), "phop")
-        for p in range(3):
-            for b in range(2):
-                add("S", lambda p=p, b=b: sca.activation(T["d3%d" % i][:, 24 * b + 8 * p:24 * b + 8 * p + 8],
-                                                         T["dn%d" % i][:, 8 * b:8 * b + 8], ACT.Copy),
-                    80.0, (("dn", i, b),), (("d3", i, p, b),))
-        n16, pp, ne, dd, ff, val = T.n16, T.pp, T.ne, T.dd, T.ff, T.val
-        ts(n16[:], T["vl%d" % i][:], 16.0, None, ALU.mult, None, 64, [("vl", i, s, b) for s in range(4) for b in range(2)], ("n16",))
-        tt(pp[:], T.phop[:, 16:64], n16[:, 0:48], ALU.add, 48, ("n16",), ("pp",), ("phop",))
-        tt(ne[:, 0:48], n16[:, 0:48], n16[:, 16:64], ALU.not_equal, 48, ("n16",), ("ne0", "nem"))
-        tt(ne[:, 48:80], n16[:, 0:32], n16[:, 32:64], ALU.not_equal, 32, ("n16",), ("ne1",))
-        tt(val[:, 0:16], n16[:, 0:16], n16[:, 48:64], ALU.not_equal, 16, ("n16",), ("val0",))
-        tt(ne[:, 16:32], ne[:, 0:16], ne[:, 16:32], ALU.mult, 16, ("ne0", "nem"), ("nem",))
-        tt(dd[:, 0:32], pp[:, 0:32], pp[:, 16:48], ALU.subtract, 32, ("pp",), ("dd",))
-        tt(ne[:, 80:96], ne[:, 48:64], ne[:, 64:80], ALU.mult, 16, ("ne1",), ("q",))
-        tt(dd[:, 0:32], dd[:, 0:32], ne[:, 0:32], ALU.mult, 32, ("dd", "ne0", "nem"), ("dd",))
-        tt(ne[:, 80:96], ne[:, 80:96], val[:, 0:16], ALU.mult, 16, ("q", "val0"), ("q",))
-        tt(ne[:, 96:112], ne[:, 16:32], ne[:, 32:48], ALU.max, 16, ("ne0", "nem"), ("x1",))
-        tt(ne[:, 112:128], ne[:, 16:32], ne[:, 32:48], ALU.min, 16, ("ne0", "nem"), ("x2",))
-        tt(ff[:, 0:32], pp[:, 16:48], dd[:, 0:32], ALU.add, 32, ("pp", "dd"), ("f0", "f1"))
-        tt(val[:, 16:32], ne[:, 80:96], ne[:, 96:112], ALU.mult, 16, ("q", "x1"), ("val1",))
-        tt(val[:, 32:48], ne[:, 80:96], ne[:, 112:128], ALU.mult, 16, ("q", "x2"), ("val2",))
-        tt(dd[:, 32:48], ff[:, 0:16], pp[:, 32:48], ALU.subtract, 16, ("f0", "pp"), ("d2",))
-        cp(ff[:, 32:48], pp[:, 32:48], 16, ("pp",), ("f2",))
-        tt(dd[:, 32:48], dd[:, 32:48], ne[:, 48:64], ALU.mult, 16, ("d2", "ne1"), ("d2",))
-        tt(ff[:, 0:16], dd[:, 32:48], pp[:, 32:48], ALU.add, 16, ("d2", "pp"), ("f0",))
-        cp(T.fi[:], ff[:], 48, ("f0", "f1", "f2"), ("fi",))
-        ts(T.uk[:, 0:48], T.fi[:], 4, None, SHR, None, 48, ("fi",), ("uk0",))
-        ts(T.uk[:, 48:96], T.fi[:], 15, None, AND, None, 48, ("fi",), ("uk1",))
-        ul, ud, dl = T["ul%d" % i], T["ud%d" % i], T["dl%d" % i]
-        cp(ul[:], T.uk[:], 96, ("uk0", "uk1"), (("ul", i),))
-        tt(ff[:], T.uk[:, 0:48], T.dm[:, 48:96], ALU.subtract, 48, ("uk0", "dm1"), ("f0", "f1", "f2"))
-        for p in range(3):
-            for b in range(2):
-                o = 16 * p + 8 * b
-                tt(ud[:, 24 * b + 8 * p:24 * b + 8 * p + 8], ff[:, o:o + 8], val[:, o:o + 8], ALU.mult, 8,
-                   ("f0", "val0", "val1", "val2"), (("ud", i, p, b),))
-        for p in range(3):
-            add("S", lambda p=p: sca.activation(dl[:, 256 * p:256 * p + 256], T.dtab[:, 0:16].indirect(ul[:, 48 + 16 * p:64 + 16 * p]), ACT.Copy),
-                10.0 + _ga(256), ("dtab", ("ul", i)), (("dl", i, p),))
+        pairs = ("01", "12", "23", "02", "13", "03")
+        lst = []
+        for q, pr in enumerate(pairs):
+            u, w = NOFF[int(pr[0])], NOFF[int(pr[1])]
+            out = pb[:, 288 + 16 * q:304 + 16 * q]
+            lst += [(out, T.ib[:], nc[:, u:u + 16], True, False), (out, T.im1[:], nc[:, w:w + 16], False, True)]
+        mm(lst, (("nc", i, 0), ("nc", i, 1), "ib", "im1"), ("pe1",))
+        ts(T.e[:], pb[:, 288:384], 0.0, None, ALU.is_equal, None, 96, (), ("e",), x=("pe1",))
+        e = {pr: 16 * q for q, pr in enumerate(pairs)}
+        mm([(pb[:, 0:288], T.ib[:], T.ct[:], True, False)], ["ib"] + ["ct%d" % q for q in range(6)], ("pe1",))
+        for (p, cand, s, lift) in ((0, 0, 0, ()), (0, 1, 1, ("01",)), (0, 2, 2, ("02",)), (1, 0, 1, ()), (1, 1, 2, ("01", "12")), (2, 0, 2, ())):
+            out = slice(48 * p + cand, 48 * p + 48, 3)
+            mm(hop("pe1", out, lambda c: T.ek[:, 48 * c + 16 * s:48 * c + 16 * s + 16], lambda c: (False, False))
+               + [(pb[:, out], T.im64[:], T.e[:, e[pr]:e[pr] + 16], False, False) for pr in lift], ("ek", "sel", "im64", "e"), ("pe1",))
+        for b in range(2):
+            for (p, cand, s, up, down) in ((0, 0, 0, ("03",), ()), (1, 0, 1, ("01", "02", "13", "03"), ()),
+                                           (1, 1, 2, ("23", "02", "03", "13"), ("01",)), (2, 0, 2, pairs, ())):
+                o = 144 + 72 * b + 24 * p
+                out = pb[:, o + cand:o + 24:3]
+                lst = [(out, T.ib[:], nc[:, NOFF[s] + 8 * b:NOFF[s] + 8 * b + 8], False, False)]
+                lst += [(out, T.im4k[:], T.e[:, e[pr] + 8 * b:e[pr] + 8 * b + 8], False, False) for pr in down]
+                lst += [(out, T.i4k[:, 0:128], T.e[:, e[pr] + 8 * b:e[pr] + 8 * b + 8], False, b == 1 and p == 2 and pr == up[-1]) for pr in up]
+                mm(lst, ("ib", "i4k0", "im4k", "e", ("nc", i, 0), ("nc", i, 1)), ("pe1",))
+        add("V", lambda: vec.tensor_tensor_scan(so[:, 0:288], T.rst2[:], pb[:, 0:288], 0.0, ALU.max, ALU.min), _v(288),
+            ("rs0", "rs1", "rs2"), (("so", i),), ("pe1",))
+        ts(ul[:], so[:, 2:288:3], CEN, None, ALU.add, None, 96, (("so", i),), (("ul", i),), 0.5)
+        add("S", lambda: sca.activation(dl[:], T.xs[:, V - int(CEN):V + 48].indirect(ul[:, 0:48]), ACT.Copy),
+            10.0 + _ga(768), ("dtab", "xs", ("ul", i)), (("dl", i),))
+        for b in (1, 0):
+            bk, o = "pe%d" % b, 146 + 72 * b
+            mm([(T[bk][:, 0:384], T.zero[:], T.zr0[:, 0:384], True, False)]
+               + [(T[bk][:, 24 * s:24 * s + 24], T.rot[:, 128 * s:128 * s + 128], so[:, o:o + 72:3], False, False) for s in range(8)],
+               [("so", i), "zero"] + zall[0] + [("rot", s) for s in range(8)], (bk,))
+            for q in range(4):
+                lst = []
+                for j in range(4 * q, 4 * q + 4):
+                    out = T[bk][:, 192 + 12 * j:204 + 12 * j]
+                    lst += [(out, T.seld[:, 128 * j:128 * j + 128], so[:, o + 3:o + 72:6], False, False),
+                            (out, T.im1[:], so[:, o:o + 72:6], False, False)]
+                mm(lst, [("so", i), "im1"] + [("seld", j) for j in range(4 * q, 4 * q + 4)], (bk,))
 
     def reinforce(i):
-        slot[0] = 6 * i + RS
         j0 = i - 1
-        ul, ud, dl = T["ul%d" % j0], T["ud%d" % j0], T["dl%d" % j0]
+        so, ul, dl = T["so%d" % j0], T["ul%d" % j0], T["dl%d" % j0]
         for b in (1, 0):
-            o, o3 = 24 * b, 36 * b
-            ww, oc, on = T.ww[:, o:o + 24], T.oc[:, o3:o3 + 36], T.on[:, o3:o3 + 36]
-            tt(ww, T["bt%d" % i][:, o:o + 24], T["d3%d" % j0][:, o:o + 24], ALU.is_lt, 24,
-               [("bt", i, b)] + [("d3", j0, p, b) for p in range(3)], (("ww", b),))
-            tt(ww, ww, ud[:, o:o + 24], ALU.mult, 24, [("ud", j0, p, b) for p in range(3)] + [("ww", b)], (("ww", b),))
-            tt(T.oc[:, o3:o3 + 24], ww, T.dm[:, 0:24], ALU.add, 24, (("ww", b), "dm0"), (("oc0", b),))
-            tt(T.on[:, o3:o3 + 24], T.dm[:, 96:120], ww, ALU.subtract, 24, (("ww", b), "dm2"), (("on0", b),))
-            ts(T.oc[:, o3 + 24:o3 + 36], T.ww[:, o + 1:o + 24:2], DUO, None, ALU.add, None, 12, (("ww", b), "duo"), (("oc1", b),))
-            ts(T.on[:, o3 + 24:o3 + 36], T.ww[:, o:o + 24:2], DUC, -1.0, ALU.add, ALU.mult, 12, (("ww", b), "duc"), (("on1", b),))
-            for q in range(2):
-                bk = "pe%d" % q
-                lst = []
-                for j in range(8):
-                    out = T[bk][:, 36 * j:36 * j + 36]
-                    lst += [(out, T.seld[:, 128 * (8 * q + j):128 * (8 * q + j + 1)], oc, True, False), (out, T.ih[:], on, False, True)]
-                mm(lst, [(n, b) for n in ("oc0", "oc1", "on0", "on1")] + ["ih"] + [("seld", 8 * q + j) for j in range(8)], (bk,))
-            for q in range(2):
-                ts(T.eq[:, 288 * q:288 * q + 288], T["pe%d" % q][:, 0:288], 0.0, None, ALU.is_equal, None, 288, (), (("eq", q),), x=("pe%d" % q,))
-            cnt = T.phop[:, 64:88]
-            mm([(cnt, T.ih[:], T.oc[:, o3:o3 + 24], True, False)], ("ih", ("oc0", b)), ("phop",))
-            for q in range(2):
-                lst = []
-                for j in range(8 * q, 8 * q + 8):
-                    lst += [(T.phop[:, 65:88:2], T.b0[:, 16 - j:144 - j], T.eq[:, 36 * j + 24:36 * j + 36], False, False),
-                            (cnt, T.lall[:, 128 * j:128 * j + 128], T.eq[:, 36 * j:36 * j + 24], False, j == 15)]
-                mm(lst, [("eq", q), "b0"] + [("lall", j) for j in range(8 * q, 8 * q + 8)], ("phop",))
-            ts(T.off[:, o:o + 24:2], T.phop[:, 64:88:2], DUC, CEN, ALU.min, ALU.add, 12, ("duc",), (("off0", b),), x=("phop",))
-            ts(T.off[:, o + 1:o + 24:2], T.phop[:, 65:88:2], DUO, CEN, ALU.min, ALU.add, 12, ("duo",), (("off1", b),), x=("phop",))
+            slot[0] = 6 * i + 6.0 - b
+            bk, o = "pe%d" % b, 24 * b
+            pb, eq, fb = T[bk], T["eq%d" % b], T["fb%d" % i][:, o:o + 24]
+            mm([(pb[:, 24 * s:24 * s + 24], T.rot[:, 128 * s:128 * s + 128], fb, False, False) for s in range(8)]
+               + [(pb[:, 192 + 12 * j:204 + 12 * j], T.ib[:], T["fb%d" % i][:, o:o + 24:2], False, j == 15) for j in range(16)],
+               (("fb", i, b), "ib"), (bk,))
+            ts(eq[:], pb[:, 0:384], 0.0, None, ALU.is_equal, None, 384, (), (("eq", b),), x=(bk,))
+            cnt = pb[:, 384:408]
+            mm([(cnt, T.ib[:], so[:, 146 + 72 * b:218 + 72 * b:3], True, False), (cnt, T.ib[:], fb, False, False)]
+               + [(cnt, T.los[:, 128 * s:128 * s + 128], eq[:, 24 * s:24 * s + 24], False, False) for s in range(8)]
+               + [(pb[:, 385:408:2], T.b0[:, 16 - j:144 - j], eq[:, 192 + 12 * j:204 + 12 * j], False, j == 15) for j in range(16)],
+               [("eq", b), "b0", "ib", ("fb", i, b), ("so", j0)] + [("los", s) for s in range(8)], (bk,))
+            ts(T.off[:, o:o + 24:2], pb[:, 384:408:2], DUC, CEN, ALU.min, ALU.add, 12, ("duc",), (("off0", b),), x=(bk,))
+            ts(T.off[:, o + 1:o + 24:2], pb[:, 385:408:2], DUO, CEN, ALU.min, ALU.add, 12, ("duo",), (("off1", b),), x=(bk,))
         for p in range(3):
-            add("V", lambda p=p: vec.tensor_tensor(T.new[:], T.ph[:, 0:V].indirect(ul[:, 16 * p:16 * p + 16]), dl[:, 256 * p:256 * p + 256], ALU.add),
-                _ga(256), ["ph", ("ul", j0), ("dl", j0, p)] + phi, ("new",))
-            ts(T.new[:], T.new[:], 0.0, 20.0, ALU.max, ALU.min, 256, ("new",), ("new",), 0.5)
+            slot[0] = 6 * i + (6.0 if p else 2.0)
+            for b in (1, 0):
+                c = 48 + 24 * b + 8 * p
+                add("V", lambda p=p, b=b, c=c: vec.tensor_tensor(T.new[:, 128 * b:128 * b + 128], T.ph[:, 0:V + 48].indirect(ul[:, c:c + 8]),
+                                                                 dl[:, 256 * p + 128 * b:256 * p + 128 * b + 128], ALU.add),
+                    _ga(128), ["ph", ("ul", j0), ("dl", j0)] + phi, (("new", b),))
+            ts(T.new[:], T.new[:], 0.0, 20.0, ALU.max, ALU.min, 256, (("new", 0), ("new", 1)), (("new", 0), ("new", 1)), 0.5)
+            slot[0] = 6 * i + 6.0
             for h in range(14, -2, -2):
                 c = 24 * (h // 8) + 8 * p + h % 8
                 add("V", lambda c=c, h=h: vec.tensor_copy(T.ph[:, 0:V + 32].indirect(T.off[:, c:c + 2]), T.new[:, 16 * h:16 * h + 32]),
-                    60.0 + 32 * SCT * CY, (("off0", h // 8), ("off1", h // 8), "new"), ("ph",))
+                    50.0 + FIX + 32 * SCT * CY, (("off0", h // 8), ("off1", h // 8), ("new", h // 8)), ("ph",))
 
     for i in range(VIS):
+        slot[0] = 6 * i + 2.0
+        if i < VIS - 1 or i > 0:
+            centre(i, 0, 8 if i else 16, 40 if i else 32, (("vl", i, 0, 0), ("vl", i, 0, 1)))
         for s in range(ST):
             for b in (1, 0):
                 step(i, s, b)
@@ -389,7 +410,7 @@ def _build(g, T, topo, core, rank):
             reinforce(i)
         if i < VIS - 1:
             trails(i)
-    cp(T.yvs[:], T["vl%d" % (VIS - 1)][:, 48:64], 16, (("vl", VIS - 1, 3, 0), ("vl", VIS - 1, 3, 1)), ("yvs",))
+    cp(T.yvs[:], T["vl%d" % (VIS - 1)][:, 72:88], 16, (("vl", VIS - 1, 3, 0), ("vl", VIS - 1, 3, 1)), ("yvs",))
     add("S", lambda: sca.dma_start(T.yv[:], T.yvs[:]), 100.0, ("yvs",), (), sem=("o_v", 16), lat=2000.0)
     add("Y", lambda: g.sync.dma_start(T.yp[:], T.ph[:, 0:V]), 100.0, ("ph",), (), sem=("o_p", 16), lat=4000.0)
     return ops, nsent[0]
@@ -435,7 +456,7 @@ def _place(ops, prio, pre):
     return st, end
 
 
-SEED, ROUNDS, JIT, SHAKES, WIN, JIT2 = 1, 60, 500.0, 13000, 2500.0, 500.0
+SEED, ROUNDS, JIT, SHAKES, WIN, JIT2 = 1, 60, 500.0, 8000, 2500.0, 500.0
 
 
 def _schedule(ops):
@@ -444,7 +465,8 @@ def _schedule(ops):
     bw = ([[] for _ in ops], [[] for _ in ops], [o["lat"] for o in ops], [0.0] * n)
     for k, o in enumerate(ops):
         for d, need in o["deps"].items():
-            lag = (ops[d]["lat"] + (HOP if o["eng"] is not None else 0.0)) if need else 0.0
+            wake = 0.0 if o["eng"] is None else OWN if o["eng"] == ops[d]["eng"] else HOP
+            lag = ops[d]["lat"] + wake if need else 0.0
             fw[0][k].append((d, ops[d]["cost"] + lag))
             fw[1][d].append(k)
             bw[0][d].append((k, o["cost"] + lag))
@@ -455,7 +477,7 @@ def _schedule(ops):
         rs, _ = _place(ops, [-(st[k] + ops[k]["cost"] + z[k]) for k in range(n)], bw)
         return [-(rs[k] + ops[k]["cost"]) for k in range(n)]
     best = None
-    prio = [o["slot"] * 3500.0 + 0.001 * k for k, o in enumerate(ops)]
+    prio = [o["slot"] * 3200.0 + 0.001 * k for k, o in enumerate(ops)]
     for it in range(ROUNDS):
         st, end = _place(ops, prio, fw)
         if best is None or end < best[1]:

@@ -1,5 +1,5 @@
+import math
 import numpy as np
-from concourse.bass import DstId, RemoteDMATransfer
 from concourse.mybir import AluOpType as ALU, ActivationFunctionType as ACT
 
 V, A, VIS, ST = 3072, 256, 4, 3
@@ -7,7 +7,7 @@ CEN = 1536.0
 SC1 = 65536.0
 BIG = 4096.0
 NONE = V - CEN + 32
-NV = [[64, 64, 64], [64, 64, 64], [16, 64, 64], [16, 64, 64]]
+NV = [[(64, 64)] * 3, [(64, 64)] * 3, [(16, 16), (64, 68), (64, 64)], [(16, 16), (64, 68), (64, 64)]]
 SPIECES = 2
 NOFF = (16, 96, 48, 72)
 F32, BF, F16, I32, U16 = "float32", "bfloat16", "float16", "int32", "uint16"
@@ -38,15 +38,15 @@ SEMAPHORES = (["cV", "cS", "cP", "cG", "sent", "l_adj", "l_x", "l_v", "l_z", "l_
               + ["r_z%d" % i for i in (1, 2, 3)]
               + ["r_%s%d%d" % (k, i, b) for k in "vf" for i in (1, 2, 3) for b in (0, 1)])
 
-CY, GA, SCT, PC, FIX, OWN, HOP = 0.9, 1.56, 3.8, 0.46, 35.0, 70.0, 140.0
+CY, GA, SCT, PC, OWN, HOP = 1.01, 1.56, 3.8, 0.51, 75.0, 140.0
 
 
 def _v(n, c=1.0):
-    return max(64.0, n * c) * CY + FIX
+    return max(64.0, n * c) * CY
 
 
-def _ga(n):
-    return 55.0 + FIX + n * GA * CY
+def _ga(n, c=GA):
+    return 61.0 + n * c * CY
 
 
 def _build(g, T, topo, core, rank):
@@ -95,34 +95,26 @@ def _build(g, T, topo, core, rank):
             return ins
         return add("P", fn, sum(max(min(64, q[0].shape[0]), q[0].shape[-1]) for q in lst) * PC, r, (), x)
 
-    def dst(c):
-        rid, pid, _ = topo.addr(c)
-        return DstId(rid=rid, pnc=pid)
-
-    def bits(es):
-        return sum(1 << e for e in es)
-
     nsent = [0]
 
-    def send(trs, r, lat, after=()):
-        nsent[0] += sum(len(t[3]) for t in trs)
+    def send(c, src, out, sem, r, w, lat, after=()):
+        rid, pid, _ = topo.addr(c)
+        ne = len(topo.engines(core, c))
+        nsent[0] += ne
 
         def fn():
-            g.remote_dma_fused([RemoteDMATransfer(dst_ids=[dst(c)], dma_engine_mask=bits(es), remote_sem=T.sem[sem],
-                                                  srcs=[s], dsts=[d]) for (c, s, d, es, sem, w) in trs], local_sem=T.sem.sent)
+            g.remote_dma(out, src, T.sem[sem], T.sem.sent, pid, rid, topo.mask(core, c))
             return None
-        n = add("G", fn, 300.0, r, (), after=after)
-        for (c, s, d, es, sem, w) in trs:
-            add(None, None, 0.0, (), w, sem=(sem, len(es)), lat=lat, after=(n,))
-        last_w["sends"] = len(ops) - 1
+        n = add("G", fn, 300.0 if "sends" in last_w else 2300.0, r, (), after=after)
+        last_w["sends"] = add(None, None, 0.0, (), w, sem=(sem, ne), lat=lat, after=(n,))
 
     def load(q, eng, out, in_, name, sem, lat):
         return add(eng, lambda: q.dma_start(out, in_), 100.0, (), (name,), ("queue" + eng,), sem=(sem, 16), lat=lat)
     load(g.sync, "Y", T.zs[:], T.z[:], "zs", "l_z", 2200.0)
-    load(sca, "S", T.v0s[:], T.v0[:], "v0s", "l_v", 2200.0)
-    load(sca, "S", T.nzs[:], T.nz[:], "nzs", "l_nz", 2400.0)
-    la = load(g.sync, "Y", T.adjs[:], T.adj[:], "adjs", "l_adj", 6500.0)
-    lx = load(sca, "S", T.xs[:, 0:V], T.x[:], "xs", "l_x", 8000.0)
+    load(g.sync, "Y", T.nzs[:], T.nz[:], "nzs", "l_nz", 2400.0)
+    load(g.sync, "Y", T.v0s[:], T.v0[:], "v0s", "l_v", 2400.0)
+    la = load(g.sync, "Y", T.adjs[:], T.adj[:], "adjs", "l_adj", 6700.0)
+    lx = load(g.sync, "Y", T.xs[:, 0:V], T.x[:], "xs", "l_x", 8800.0)
 
     def iota(out, pat, name, base=0):
         add("G", lambda: g.iota(out, pat, base, 0, allow_small_or_imprecise_dtypes=True), 130.0 + 1.8 * out.shape[-1], (), (name,))
@@ -172,7 +164,7 @@ def _build(g, T, topo, core, rank):
 
     def wishes(i, after):
         c = T.cores[(rank + i) % len(T.cores)]
-        send([(c, T.zr0[:], T["zr%d" % i][:], topo.engines(core, c), "r_z%d" % i, zall[i])], zall[0], 6000.0, after=after)
+        send(c, T.zr0[:], T["zr%d" % i][:], "r_z%d" % i, zall[0], zall[i], 6000.0, after)
     wishes(1, (la, lx))
     slot[0] = -1.0
     ts(T.rq[:, 2:24:3], T.rq[:, 2:24:3], HB8, 64.0, ALU.add, ALU.add, 8, ("rq0", "hb8"), ("rq0",))
@@ -219,7 +211,7 @@ def _build(g, T, topo, core, rank):
     def step(i, s, b):
         t = ST * i + s
         last = s == ST - 1
-        nv = NV[i][s]
+        nv = NV[i][s][b]
         W = 256 if last else 128
         vl, zr = T["vl%d" % i], T["zr%d" % i]
         nm, nf, pg, a1, a2, e1, pk = (T["%s%d" % (n, b)] for n in ("nm", "nf", "pg", "a1", "a2", "e1", "pk"))
@@ -242,10 +234,9 @@ def _build(g, T, topo, core, rank):
             n1, n2 = ("a1", b, pn), ("a2", b, pn)
             add("S", lambda c0=c0, c1=c1: sca.activation(a2[:, 16 * c0:16 * c1], T.xs[:, 0:V].indirect(nm[:, c0:c1]), ACT.Copy),
                 10.0 + _ga(n), ("xs", ("nm", b)), (n2, ("a2", b, "v")) if c0 == 0 else (n2,))
-            for o in range(0, n, 512):
-                e = min(n, o + 512)
-                mm([(pd[:, o:e], T.ib[:], zr[:, 2048 * b + 16 * c0 + o:2048 * b + 16 * c0 + e], True, False),
-                    (pd[:, o:e], T.ib[:], a2[:, 16 * c0 + o:16 * c0 + e], False, True)], ["ib", n2] + zall[i], (pn,))
+            banks = [(o, min(n, o + 512)) for o in range(0, n, 512)]
+            mm([(pd[:, o:e], T.ib[:], zr[:, 2048 * b + 16 * c0 + o:2048 * b + 16 * c0 + e], True, False) for o, e in banks], ["ib"] + zall[i], (pn,))
+            mm([(pd[:, o:e], T.ib[:], a2[:, 16 * c0 + o:16 * c0 + e], False, True) for o, e in banks], ("ib", n2), (pn,))
             add("S", lambda c0=c0, c1=c1, pd=pd, n=n: sca.activation(a1[:, 16 * c0:16 * c1], pd[:, 0:n], ACT.Abs, scale=0.5),
                 _v(n), (), (n1, ("a1", b, "v")) if c0 == 0 else (n1,), (pn,))
             a1n.append(n1)
@@ -285,34 +276,27 @@ def _build(g, T, topo, core, rank):
         el = T.el[:, 4:12] if last else T.el[:, 0:4]
         add("V", lambda: vec.tensor_scalar(e1[:, 0:64 * nq], T.wn[:, wn:wn + 24].indirect(el), CEN, None, ALU.subtract),
             _ga(64 * nq), ("wn%d" % b, "wd%d" % b, "el0"), (("e1", b),))
-        lst2 = hop(bank, slice(256, 256 + 8 * nq), lambda c: e1[:, 8 * nq * c:8 * nq * (c + 1)], lambda c: (c % 2 == 0, c % 2 == 1))
-        rd = [("e1", b), "sel"]
-        if last and i > 0:
-            dp = T["nc%d" % i][:, 8 + 24 * b:16 + 24 * b]
-            for p in range(3):
-                o = 272 + 8 * p
-                lst2.append((pk[:, o:o + 8], T.im1[:], dp, True, False))
-                lst2 += hop(bank, slice(o, o + 8), lambda c: e1[:, 16 * c + k2 // 16:16 * c + k2 // 16 + 8], lambda c: (False, c % 2 == 1))
-            rd += ["im1", ("nc", i, 0)]
-        mm(lst2, rd, (bank,))
-        o = 64 + 16 * b if last else NOFF[s + 1] + 8 * b
-        if last and i > 0:
+
+        def nodes():
+            mm(hop(bank, slice(256, 256 + 8 * nq), lambda c: e1[:, 8 * nq * c:8 * nq * (c + 1)], lambda c: (c % 2 == 0, c % 2 == 1)),
+               (("e1", b), "sel"), (bank,))
+            o = 64 + 16 * b if last else NOFF[s + 1] + 8 * b
+            ts(vl[:, o:o + 8 * nq], pk[:, 256:256 + 8 * nq], CEN, None, ALU.add, None, 8, (), (("vl", i, s + 1, b),), x=(bank,))
+            if last and i < VIS - 1:
+                send(nxt, vl[:, o:o + 16], T["vl%d" % (i + 1)][:, 8 + 16 * b:24 + 16 * b], "r_v%d%d" % (i + 1, b),
+                     (("vl", i, 3, b),), (("vl", i + 1, 0, b),), 2100.0)
+
+        def flags():
+            dp, lst = T["nc%d" % i][:, 8 + 24 * b:16 + 24 * b], []
+            for o in (272, 280, 288):
+                lst.append((pk[:, o:o + 8], T.im1[:], dp, True, False))
+                lst += hop(bank, slice(o, o + 8), lambda c: e1[:, 16 * c + k2 // 16:16 * c + k2 // 16 + 8], lambda c: (False, c % 2 == 1))
+            mm(lst, (("e1", b), "sel", "im1", ("nc", i, 0)), (bank,))
             fo = T["fo%d" % i][:, 24 * b:24 * b + 24]
             ts(fo, pk[:, 272:296], 0.0, BIG, ALU.is_ge, ALU.mult, 24, (), (("fo", i, b),), x=(bank,))
-        ts(vl[:, o:o + 8 * nq], pk[:, 256:256 + 8 * nq], CEN, None, ALU.add, None, 8, (), (("vl", i, s + 1, b),), x=(bank,))
-        if last:
-            trs, rd = [], []
-            e_n, e_p = topo.engines(core, nxt), topo.engines(core, prv)
-            if 0 < i < VIS - 1:
-                e_n, e_p = e_n[:len(e_n) // 2], e_p[len(e_p) // 2:]
-            if i < VIS - 1:
-                trs.append((nxt, vl[:, 56 + 24 * b:80 + 24 * b], T["vl%d" % (i + 1)][:, 24 * b:24 * b + 24], e_n,
-                            "r_v%d%d" % (i + 1, b), (("vl", i + 1, 0, b),)))
-                rd += [("vl", i, 3, b), ("vl", i, 2 - b, 1 - b)]
-            if i > 0:
-                trs.append((prv, fo, T["fb%d" % i][:, 24 * b:24 * b + 24], e_p, "r_f%d%d" % (i, b), (("fb", i, b),)))
-                rd.append(("fo", i, b))
-            send(trs, rd, 1800.0)
+            send(prv, fo, T["fb%d" % i][:, 24 * b:24 * b + 24], "r_f%d%d" % (i, b), (("fo", i, b),), (("fb", i, b),), 2100.0)
+        for part in ((nodes,) if not last or i == 0 else (nodes, flags) if b == 1 and i < VIS - 1 else (flags, nodes)):
+            part()
 
     def centre(i, q, lo, hi, r):
         ts(T["nc%d" % i][:, lo:hi], T["vl%d" % i][:, lo:hi], CEN, None, ALU.subtract, None, hi - lo, r, (("nc", i, q),), 0.5)
@@ -340,7 +324,7 @@ def _build(g, T, topo, core, rank):
                + [(pb[:, out], T.im64[:], T.e[:, e[pr]:e[pr] + 16], False, False) for pr in lift], ("ek", "sel", "im64", "e"), ("pe1",))
         for b in range(2):
             for (p, cand, s, up, down) in ((0, 0, 0, ("03",), ()), (1, 0, 1, ("01", "02", "13", "03"), ()),
-                                           (1, 1, 2, ("23", "02", "03", "13"), ("01",)), (2, 0, 2, pairs, ())):
+                                           (1, 1, 2, ("23", "02", "03"), ("01",)), (2, 0, 2, pairs, ())):
                 o = 144 + 72 * b + 24 * p
                 out = pb[:, o + cand:o + 24:3]
                 lst = [(out, T.ib[:], nc[:, NOFF[s] + 8 * b:NOFF[s] + 8 * b + 8], False, False)]
@@ -353,34 +337,36 @@ def _build(g, T, topo, core, rank):
         add("S", lambda: sca.activation(dl[:], T.xs[:, V - int(CEN):V + 48].indirect(ul[:, 0:48]), ACT.Copy),
             10.0 + _ga(768), ("dtab", "xs", ("ul", i)), (("dl", i),))
         for b in (1, 0):
-            bk, o = "pe%d" % b, 146 + 72 * b
-            mm([(T[bk][:, 0:384], T.zero[:], T.zr0[:, 0:384], True, False)]
-               + [(T[bk][:, 24 * s:24 * s + 24], T.rot[:, 128 * s:128 * s + 128], so[:, o:o + 72:3], False, False) for s in range(8)],
-               [("so", i), "zero"] + zall[0] + [("rot", s) for s in range(8)], (bk,))
+            o = 146 + 72 * b
             for q in range(4):
                 lst = []
                 for j in range(4 * q, 4 * q + 4):
-                    out = T[bk][:, 192 + 12 * j:204 + 12 * j]
-                    lst += [(out, T.seld[:, 128 * j:128 * j + 128], so[:, o + 3:o + 72:6], False, False),
-                            (out, T.im1[:], so[:, o:o + 72:6], False, False)]
-                mm(lst, [("so", i), "im1"] + [("seld", j) for j in range(4 * q, 4 * q + 4)], (bk,))
+                    out = pb[:, 192 * b + 12 * j:192 * b + 12 * j + 12]
+                    lst += [(out, T.seld[:, 128 * j:128 * j + 128], so[:, o + 3:o + 72:6], True, False),
+                            (out, T.im1[:], so[:, o:o + 72:6], False, True)]
+                mm(lst, [("so", i), "im1"] + [("seld", j) for j in range(4 * q, 4 * q + 4)], ("pe1",))
 
     def reinforce(i):
         j0 = i - 1
         so, ul, dl = T["so%d" % j0], T["ul%d" % j0], T["dl%d" % j0]
         for b in (1, 0):
             slot[0] = 6 * i + 6.0 - b
-            bk, o = "pe%d" % b, 24 * b
+            bk, o = "pe1", 24 * b
             pb, eq, fb = T[bk], T["eq%d" % b], T["fb%d" % i][:, o:o + 24]
-            mm([(pb[:, 24 * s:24 * s + 24], T.rot[:, 128 * s:128 * s + 128], fb, False, False) for s in range(8)]
-               + [(pb[:, 192 + 12 * j:204 + 12 * j], T.ib[:], T["fb%d" % i][:, o:o + 24:2], False, j == 15) for j in range(16)],
-               (("fb", i, b), "ib"), (bk,))
-            ts(eq[:], pb[:, 0:384], 0.0, None, ALU.is_equal, None, 384, (), (("eq", b),), x=(bk,))
+            ub = so[:, 146 + 72 * b:218 + 72 * b:3]
+            for first, rhs, r in ((True, ub, ("so", j0)), (False, fb, ("fb", i, b))):
+                mm([(T.pe0[:, 24 * s:24 * s + 24], T.rot[:, 128 * s:128 * s + 128], rhs, first and s == 0, not first and s == 7)
+                    for s in range(8)], [r] + [("rot", s) for s in range(8)], ("pe0",))
+            for h in range(4):
+                ts(eq[:, 192 + h:384:4], pb[:, 192 * b + h:192 * b + 192:4], fb[:, 2 * h:2 * h + 1], None, ALU.is_equal, None, 48,
+                   (("fb", i, b),), (("eqx", b, h),), x=(bk,))
+            ts(eq[:, 0:192], T.pe0[:, 0:192], 0.0, None, ALU.is_equal, None, 192, (), (("eq", b),), x=("pe0",))
             cnt = pb[:, 384:408]
-            mm([(cnt, T.ib[:], so[:, 146 + 72 * b:218 + 72 * b:3], True, False), (cnt, T.ib[:], fb, False, False)]
-               + [(cnt, T.los[:, 128 * s:128 * s + 128], eq[:, 24 * s:24 * s + 24], False, False) for s in range(8)]
-               + [(pb[:, 385:408:2], T.b0[:, 16 - j:144 - j], eq[:, 192 + 12 * j:204 + 12 * j], False, j == 15) for j in range(16)],
-               [("eq", b), "b0", "ib", ("fb", i, b), ("so", j0)] + [("los", s) for s in range(8)], (bk,))
+            mm([(cnt, T.ib[:], ub, True, False), (cnt, T.ib[:], fb, False, False)]
+               + [(pb[:, 385:408:2], T.b0[:, 16 - j:144 - j], eq[:, 192 + 12 * j:204 + 12 * j], False, False) for j in range(16)],
+               [("eqx", b, h) for h in range(4)] + ["b0", "ib", ("fb", i, b), ("so", j0)], (bk,))
+            mm([(cnt, T.los[:, 128 * s:128 * s + 128], eq[:, 24 * s:24 * s + 24], False, s == 7) for s in range(8)],
+               [("eq", b)] + [("los", s) for s in range(8)], (bk,))
             ts(T.off[:, o:o + 24:2], pb[:, 384:408:2], DUC, CEN, ALU.min, ALU.add, 12, ("duc",), (("off0", b),), x=(bk,))
             ts(T.off[:, o + 1:o + 24:2], pb[:, 385:408:2], DUO, CEN, ALU.min, ALU.add, 12, ("duo",), (("off1", b),), x=(bk,))
         for p in range(3):
@@ -390,12 +376,14 @@ def _build(g, T, topo, core, rank):
                 add("V", lambda p=p, b=b, c=c: vec.tensor_tensor(T.new[:, 128 * b:128 * b + 128], T.ph[:, 0:V + 48].indirect(ul[:, c:c + 8]),
                                                                  dl[:, 256 * p + 128 * b:256 * p + 128 * b + 128], ALU.add),
                     _ga(128), ["ph", ("ul", j0), ("dl", j0)] + phi, (("new", b),))
-            ts(T.new[:], T.new[:], 0.0, 20.0, ALU.max, ALU.min, 256, (("new", 0), ("new", 1)), (("new", 0), ("new", 1)), 0.5)
+            for b in (1, 0):
+                nw = T.new[:, 128 * b:128 * b + 128]
+                ts(nw, nw, 0.0, 20.0, ALU.max, ALU.min, 128, (("new", b),), (("new", b),), 0.5)
             slot[0] = 6 * i + 6.0
             for h in range(14, -2, -2):
                 c = 24 * (h // 8) + 8 * p + h % 8
                 add("V", lambda c=c, h=h: vec.tensor_copy(T.ph[:, 0:V + 32].indirect(T.off[:, c:c + 2]), T.new[:, 16 * h:16 * h + 32]),
-                    50.0 + FIX + 32 * SCT * CY, (("off0", h // 8), ("off1", h // 8), ("new", h // 8)), ("ph",))
+                    _ga(32, SCT), (("off0", h // 8), ("off1", h // 8), ("new", h // 8)), ("ph",))
 
     for i in range(VIS):
         slot[0] = 6 * i + 2.0
@@ -456,7 +444,7 @@ def _place(ops, prio, pre):
     return st, end
 
 
-SEED, ROUNDS, JIT, SHAKES, WIN, JIT2 = 1, 60, 500.0, 8000, 2500.0, 500.0
+SEED, ROUNDS, JIT, SHAKES, SWEEPS, WIN, MOVES, HOT, COLD, REACH = 1, 20, 500.0, 30000, 8, 300, 8000, 500.0, 50.0, 1.2
 
 
 def _schedule(ops):
@@ -483,16 +471,119 @@ def _schedule(ops):
         if best is None or end < best[1]:
             best = (st, end)
         prio = back(best[0] if it % 4 == 3 else st, (rng.random(n) * (JIT if it % 2 else 0.0)).tolist())
-    st, end = best
-    cur = np.array(st)
-    for it in range(SHAKES):
-        m = np.abs(cur - rng.random() * end) < WIN * (0.3 + rng.random())
-        s2, e2 = _place(ops, (cur + m * rng.normal(0.0, 1.0, n) * (JIT2 * (0.2 + rng.random()))).tolist(), fw)
-        if it % 8 == 7:
-            s2, e2 = _place(ops, back(s2, [0.0] * n), fw)
-        if e2 <= end:
-            cur, end, st = np.array(s2), e2, s2
-    return sorted(range(n), key=lambda k: (st[k], k)), st, end
+    return _anneal(ops, sorted(range(n), key=lambda k: (best[0][k], k)), fw, rng)
+
+
+def _anneal(ops, order, pre, rng):
+    n = len(ops)
+    names = sorted(set(o["eng"] for o in ops if o["eng"] is not None))
+    eng = [names.index(o["eng"]) if o["eng"] is not None else -1 for o in ops]
+    cost = [o["cost"] for o in ops]
+    pred, succ = pre[0], pre[1]
+    preds = [[d for d, lag in p] for p in pred]
+
+    def run(seq, lo, free, st, by):
+        free, who = free[:], [-1] * len(names)
+        for k in seq[max(0, lo - 150):lo]:
+            if eng[k] >= 0:
+                free[eng[k]], who[eng[k]] = st[k] + cost[k], k
+        for k in seq[lo:]:
+            t, w = 0.0, -1
+            for d, lag in pred[k]:
+                x = st[d] + lag
+                if x > t:
+                    t = x
+                    w = d
+            e = eng[k]
+            if e >= 0:
+                if free[e] > t:
+                    t = free[e]
+                    w = -2 - who[e]
+                free[e] = t + cost[k]
+                who[e] = k
+            st[k] = t
+            by[k] = w
+        return free
+
+    def window(order, lo, hi, moves):
+        st, by = [0.0] * n, [-1] * n
+        free = run(order[:lo], 0, [0.0] * len(names), st, by)
+        rest, behind = [0.0] * n, [0.0] * len(names)
+        for k in reversed(order[hi:]):
+            rest[k] = max(rest[k], cost[k] + ops[k]["lat"])
+            if eng[k] >= 0:
+                rest[k] = behind[eng[k]] = max(rest[k], cost[k] + behind[eng[k]])
+            for d, lag in pred[k]:
+                rest[d] = max(rest[d], lag + rest[k])
+        seq = order[lo:hi]
+        inside = set(seq)
+        ends = [k for k in seq if rest[k] or not succ[k]]
+        for k in ends:
+            rest[k] = max(rest[k], cost[k] + ops[k]["lat"])
+
+        def look(seq, a, st, by):
+            last = run(seq, a, free, st, by)
+            end, k = max([(st[k] + rest[k], k) for k in ends])
+            for e, t in enumerate(last):
+                if t + behind[e] > end and t > free[e]:
+                    end, k = t + behind[e], [q for q in seq if eng[q] == e][-1]
+            return end, k
+
+        def chain(k, by):
+            out = []
+            d = by[k]
+            while d != -1:
+                if d < -1:
+                    d = -2 - d
+                    out.append((d, k))
+                if d not in inside:
+                    break
+                k = d
+                d = by[k]
+            return out
+        end, k = look(seq, 0, st, by)
+        arcs, best, m = chain(k, by), (end, seq), len(seq)
+        for it, r in enumerate(rng.random((moves, 4)).tolist()):
+            if not arcs:
+                break
+            u, v = arcs[int(r[0] * len(arcs))]
+            a, b = seq.index(u), seq.index(v)
+            e, more, up = eng[u], int(-math.log(1.0 - r[2]) * REACH), r[1] < 0.5
+            if up:
+                while more and a > 0:
+                    a -= 1
+                    more -= eng[seq[a]] == e
+                seg, mark, need = seq[a:b + 1], {v}, set(preds[v])
+            else:
+                while more and b < m - 1:
+                    b += 1
+                    more -= eng[seq[b]] == e
+                seg, mark, need = seq[a:b + 1], {u}, set(succ[u])
+            qs = set()
+            for k in (seg[-2::-1] if up else seg[1:]):
+                if k in need or eng[k] in qs:
+                    mark.add(k)
+                    need.update(preds[k] if up else succ[k])
+                    if eng[k] != e and eng[k] >= 0:
+                        qs.add(eng[k])
+            if u in mark and v in mark:
+                continue
+            q2 = seq[:a] + [k for k in seg if (k in mark) == up] + [k for k in seg if (k in mark) != up] + seq[b + 1:]
+            s2, b2 = st[:], by[:]
+            e2, k = look(q2, a, s2, b2)
+            if e2 <= end - HOT * (COLD / HOT) ** (it / moves) * math.log(1.0 - r[3]):
+                seq, st, by, end = q2, s2, b2, e2
+                arcs = chain(k, by)
+                if it % 64 == 0:
+                    seq = sorted(seq, key=lambda k: st[k])
+                if end < best[0]:
+                    best = (end, seq)
+        return order[:lo] + best[1] + order[hi:], best[0]
+    order, end = window(order, 0, n, SHAKES)
+    for sweep in range(SWEEPS):
+        for lo in range(-int(rng.random() * WIN / 2), n - WIN // 3, WIN // 2):
+            order, end = window(order, max(0, lo), min(n, lo + WIN), MOVES)
+    return order, None, window(order, 0, n, 0)[1]
 
 
 _ORDER = {}

import math
import numpy as np
from concourse.mybir import AluOpType as ALU, ActivationFunctionType as ACT

V, A, VIS, ST = 3072, 256, 4, 3
CEN = 1536.0
SC1 = 65536.0
BIG = 4096.0
NONE = V - CEN + 32
NV = [[(64, 64)] * 3, [(64, 64)] * 3, [(16, 16), (64, 68), (64, 64)], [(16, 16), (64, 68), (64, 64)]]
SPIECES = 2
NOFF = (16, 96, 48, 72)
F32, BF, F16, I32, U16 = "float32", "bfloat16", "float16", "int32", "uint16"

_SB = {
    "adjs": (V, I32), "xs": (V + 48, BF), "ph": (V + 48, BF), "v0s": (16, I32), "zs": (A, BF), "nzs": (A, BF), "nzk": (A + 16, F16),
    "rb": (144, BF), "rm": (256, F32), "rq": (48, F32), "pi": (8, I32), "pf": (16, F32), "tg": (48, F32),
    "zero": (128, BF), "ib": (128, BF), "i4k": (256, BF), "i65": (256, BF), "i2": (128, BF), "i32": (128, BF), "im1": (128, BF),
    "im64": (128, BF), "im4k": (128, BF), "c1": (16, BF), "c2": (16, BF), "rst": (256, BF), "sel": (48, BF), "b0": (144, BF),
    "seld": (2048, BF), "rot": (1024, BF), "los": (1024, BF), "ct": (288, BF), "rst2": (288, BF),
    "elf": (40, F32), "el": (40, U16), "sc": (1024, I32), "wn": (48, I32), "w2": (72, I32), "k2": (16, I32), "ek": (384, F16),
    "e": (96, BF), "off": (48, U16), "new": (256, BF), "yvs": (16, F32),
}
for _i in range(VIS):
    _SB.update({"zr%d" % _i: (16 * A, BF), "vl%d" % _i: (112, U16), "nc%d" % _i: (112, F16)})
    if _i > 0:
        _SB.update({"fo%d" % _i: (48, BF), "fb%d" % _i: (48, BF)})
    if _i < VIS - 1:
        _SB.update({"so%d" % _i: (296, F16), "ul%d" % _i: (96, U16), "dl%d" % _i: (768, BF)})
for _b in range(2):
    _SB.update({"nm%d" % _b: (128, U16), "nf%d" % _b: (128, F16), "pg%d" % _b: (128, BF), "a1%d" % _b: (2048, BF),
                "a2%d" % _b: (2048, BF), "e1%d" % _b: (128, F16), "eq%d" % _b: (384, BF)})
SCRATCH = {_n: ("sbuf", [128, _w], _d) for _n, (_w, _d) in _SB.items()}
for _n, _w in (("pd0", 1024), ("pd1", 1024), ("pk0", 512), ("pk1", 512), ("pe0", 512), ("pe1", 512)):
    SCRATCH[_n] = ("psum", [128, _w], F32)

SEMAPHORES = (["cV", "cS", "cP", "cG", "sent", "l_adj", "l_x", "l_v", "l_z", "l_nz", "o_p", "o_v"]
              + ["r_z%d" % i for i in (1, 2, 3)]
              + ["r_%s%d%d" % (k, i, b) for k in "vf" for i in (1, 2, 3) for b in (0, 1)])

CY, GA, SCT, PC, OWN, HOP = 1.01, 1.56, 3.8, 0.51, 75.0, 140.0


def _v(n, c=1.0):
    return max(64.0, n * c) * CY


def _ga(n, c=GA):
    return 61.0 + n * c * CY


def _build(g, T, topo, core, rank):
    ops = []
    last_w, readers = {}, {}
    slot = [-9.0]
    nxt, prv = T.cores[(rank + 1) % len(T.cores)], T.cores[(rank - 1) % len(T.cores)]
    vec, sca, pe = g.vector, g.scalar, g.tensor

    def add(eng, fn, cost, r=(), w=(), x=(), sem=None, lat=0.0, after=()):
        n = len(ops)
        deps = {}
        for d in after:
            deps[d] = True
        for k in r:
            if k in last_w:
                deps[last_w[k]] = True
        for k in tuple(w) + tuple(x):
            for d in ([last_w[k]] if k in last_w else []) + readers.get(k, []):
                deps[d] = deps.get(d, False) or ops[d]["eng"] != eng or k not in x
        for k in r:
            readers.setdefault(k, []).append(n)
        for k in tuple(w) + tuple(x):
            last_w[k] = n
            readers[k] = []
        deps.pop(n, None)
        ops.append({"eng": eng, "fn": fn, "cost": cost, "deps": deps, "sem": sem, "lat": lat, "slot": slot[0]})
        return n

    def ts(out, in0, s1, s2, o0, o1, n, r, w, c=1.0, x=()):
        if o1 is None:
            return add("V", lambda: vec.tensor_scalar(out, in0, s1, None, o0), _v(n, c), r, w, x)
        return add("V", lambda: vec.tensor_scalar(out, in0, s1, s2, o0, o1), _v(n, c), r, w, x)

    def tt(out, a, b, op, n, r, w, x=()):
        return add("V", lambda: vec.tensor_tensor(out, a, b, op), _v(n, 1.0 if x else 2.0), r, w, x)

    def cp(out, a, n, r, w, x=(), cost=None):
        return add("V", lambda: vec.tensor_copy(out, a), cost or _v(n), r, w, x)

    def mm(lst, r, x):
        def fn():
            ins = None
            for (o, l, rh, st, sp) in lst:
                ins = pe.matmul(o, l, rh, st, sp)
            return ins
        return add("P", fn, sum(max(min(64, q[0].shape[0]), q[0].shape[-1]) for q in lst) * PC, r, (), x)

    nsent = [0]

    def send(c, src, out, sem, r, w, lat, after=()):
        rid, pid, _ = topo.addr(c)
        ne = len(topo.engines(core, c))
        nsent[0] += ne

        def fn():
            g.remote_dma(out, src, T.sem[sem], T.sem.sent, pid, rid, topo.mask(core, c))
            return None
        n = add("G", fn, 300.0 if "sends" in last_w else 2300.0, r, (), after=after)
        last_w["sends"] = add(None, None, 0.0, (), w, sem=(sem, ne), lat=lat, after=(n,))

    def load(q, eng, out, in_, name, sem, lat):
        return add(eng, lambda: q.dma_start(out, in_), 100.0, (), (name,), ("queue" + eng,), sem=(sem, 16), lat=lat)
    load(g.sync, "Y", T.zs[:], T.z[:], "zs", "l_z", 2200.0)
    load(g.sync, "Y", T.nzs[:], T.nz[:], "nzs", "l_nz", 2400.0)
    load(g.sync, "Y", T.v0s[:], T.v0[:], "v0s", "l_v", 2400.0)
    la = load(g.sync, "Y", T.adjs[:], T.adj[:], "adjs", "l_adj", 6700.0)
    lx = load(g.sync, "Y", T.xs[:, 0:V], T.x[:], "xs", "l_x", 8800.0)

    def iota(out, pat, name, base=0):
        add("G", lambda: g.iota(out, pat, base, 0, allow_small_or_imprecise_dtypes=True), 130.0 + 1.8 * out.shape[-1], (), (name,))

    def mark(out, in_, pat, fill, base, r, name):
        add("G", lambda: g.affine_select(out, in_, pat, ALU.not_equal, fill, base, 1), 170.0 + 1.8 * out.shape[-1], r, (name,))
    add("G", lambda: g.iota(T.pi[:, 0:1], [[0, 1]], 0, 1), 130.0, (), ("pi0",))
    iota(T.rb[:], [[1, 144]], "rb")
    iota(T.rq[:, 0:24], [[1, 8], [16, 3]], "rq0")
    iota(T.rq[:, 24:40], [[0, 2], [1, 8]], "rq1")
    iota(T.rm[:], [[0, 16], [1, 16]], "rm")
    AND, SHR = ALU.bitwise_and, ALU.logical_shift_right
    ts(T.pi[:, 1:2], T.pi[:, 0:1], 15, None, AND, None, 1, ("pi0",), ("pi1",))
    ts(T.pi[:, 2:3], T.pi[:, 0:1], 4, None, SHR, None, 1, ("pi0",), ("pi2",))
    ts(T.pi[:, 3:4], T.pi[:, 0:1], 7, None, AND, None, 1, ("pi0",), ("pi3",))
    ts(T.pi[:, 4:5], T.pi[:, 0:1], 3, 1, SHR, AND, 1, ("pi0",), ("pi4",))
    cp(T.pf[:, 0:5], T.pi[:, 0:5], 5, ("pi0", "pi1", "pi2", "pi3", "pi4"), ("pf",))
    P, PM, PG, P7, HB, COND, KK, KH, DUC, DUO, HB1, HB2, HB8, G16 = (T.pf[:, k:k + 1] for k in range(14))
    tt(COND, P7, PG, ALU.is_equal, 1, ("pf",), ("cond",))
    for (col, src, m, a, name) in ((KK, PM, -1.0, 15.0, "kk"), (KH, PM, -1.0, 15.5, "kh"), (DUC, PM, 1.0, V - CEN, "duc"),
                                   (DUO, PM, 1.0, V - CEN + 16, "duo"), (HB1, HB, 1.0, -16.0, "hb1"), (HB2, HB, 8.0, -16.0, "hb2"),
                                   (HB8, HB, 8.0, -64.0, "hb8"), (G16, PG, 16.0, 16.0, "g16")):
        add("S", lambda col=col, src=src, m=m, a=a: sca.activation(col, src, ACT.Copy, bias=a, scale=m), _v(1), ("pf",), (name,))
    ts(T.ib[:], T.rb[:, 0:128], P, None, ALU.is_equal, None, 128, ("rb", "pf"), ("ib",), 0.5)
    for (out, m, name) in ((T.i4k[:, 0:128], BIG, "i4k0"), (T.i4k[:, 128:256], BIG, "i4k1"), (T.i2[:], 2.0, "i2"), (T.im1[:], -1.0, "im1"),
                           (T.zero[:], 0.0, "zero"), (T.i65[:, 0:128], SC1, "i650"), (T.i65[:, 128:256], SC1, "i651"),
                           (T.i32[:], 32.0, "i32"), (T.im64[:], -64.0, "im64"), (T.im4k[:], -BIG, "im4k")):
        ts(out, T.ib[:], m, None, ALU.mult, None, 128, ("ib",), (name,), 0.5)
    ts(T.c1[:], T.rq[:, 24:40], PG, -2.0 * SC1, ALU.is_equal, ALU.mult, 16, ("rq1", "pf"), ("c1",))
    ts(T.c2[:], T.rq[:, 24:40], PG, SC1, ALU.is_equal, ALU.mult, 16, ("rq1", "pf"), ("c2",))
    ts(T.rst[:], T.rm[:], 0.0, -67108864.0, ALU.is_equal, ALU.mult, 256, ("rm",), ("rst",))
    ts(T.sel[:], T.rb[:, 0:48], PM, 16.0, ALU.subtract, ALU.is_equal, 48, ("rb", "pf"), ("sel",))
    ts(T.nzk[:, 0:A], T.nzs[:], 16.0, KH, ALU.mult, ALU.add, A, ("nzs", "kh"), ("nzk0",), 0.5)
    ts(T.nzk[:, A:A + 16], T.nzs[:, 0:16], 16.0, KH, ALU.mult, ALU.add, 16, ("nzs", "kh"), ("nzk1",))
    ts(T.elf[:, 0:4], T.rb[:, 0:8:2], HB1, COND, ALU.add, ALU.mult, 4, ("rb", "hb1", "cond"), ("elf0",))
    ts(T.elf[:, 4:12], T.rb[:, 0:8], HB2, COND, ALU.add, ALU.mult, 8, ("rb", "hb2", "cond"), ("elf1",))
    ts(T.el[:, 0:12], T.elf[:, 0:12], 16.0, None, ALU.add, None, 12, ("elf0", "elf1"), ("el0",))
    add("V", lambda: vec.memset(T.wn[:], int(CEN)), _v(48), (), ("wn0", "wn1", "wd0", "wd1"))
    cp(T.vl0[:, 16:32], T.v0s[:], 16, ("v0s",), (("vl", 0, 0, 0), ("vl", 0, 0, 1)))
    for k in range(16):
        if k % 2:
            add("S", lambda k=k: sca.activation(T.zr0[:, k::16], T.zs[:], ACT.Copy, scale=-1.0), _v(A), ("zs",), (("zr", 0, k),))
        else:
            ts(T.zr0[:, k::16], T.zs[:], -1.0, None, ALU.mult, None, A, ("zs",), (("zr", 0, k),), 0.5)
    zall = {i: [("zr", i, 0)] for i in range(1, VIS)}
    zall[0] = [("zr", 0, k) for k in range(16)]

    def wishes(i, after):
        c = T.cores[(rank + i) % len(T.cores)]
        send(c, T.zr0[:], T["zr%d" % i][:], "r_z%d" % i, zall[0], zall[i], 6000.0, after)
    wishes(1, (la, lx))
    slot[0] = -1.0
    ts(T.rq[:, 2:24:3], T.rq[:, 2:24:3], HB8, 64.0, ALU.add, ALU.add, 8, ("rq0", "hb8"), ("rq0",))
    ts(T.elf[:, 12:36], T.rq[:, 0:24], HB8, COND, ALU.add, ALU.mult, 24, ("rq0", "hb8", "cond"), ("elf2",))
    ts(T.el[:, 12:36], T.elf[:, 12:36], 64.0, None, ALU.add, None, 24, ("elf2",), ("el1",))
    add("V", lambda: vec.memset(T.w2[:], 0), _v(72), (), ("w2k",))
    ts(T.xs[:, V:V + 48], T.rm[:, 0:48], KK, 11.0, ALU.is_equal, ALU.mult, 48, ("rm", "kk"), ("dtab",))
    ts(T.xs[:, V:V + 48], T.xs[:, V:V + 48], -3.0, None, ALU.add, None, 48, ("dtab",), ("dtab",))
    sr, tr_, tl = T.rb[:, 1:9], T.tg[:, 0:8], T.tg[:, 8:16]
    ts(tr_, sr, PM, 16.0, ALU.is_gt, ALU.mult, 8, ("rb", "pf"), ("tr",))
    tt(tr_, tr_, sr, ALU.subtract, 8, ("tr", "rb"), ("tr",))
    ts(tr_, tr_, P, None, ALU.add, None, 8, ("tr", "pf"), ("tr",))
    ts(tl, sr, KK, None, ALU.is_le, None, 8, ("rb", "kk"), ("tl",))
    tt(tl, tl, sr, ALU.mult, 8, ("tl", "rb"), ("tl",))
    ts(tl, tl, P, None, ALU.add, None, 8, ("tl", "pf"), ("tl",))
    for s in range(8):
        o = 128 * s
        ts(T.rot[:, o:o + 128], T.rb[:, 0:128], T.tg[:, s:s + 1], None, ALU.is_equal, None, 128, ("rb", "tr"), (("rot", s),), 0.5)
        mark(T.rot[:, o:o + 128], T.rot[:, o:o + 128], [[-1, 128]], -1.0, 0, (("rot", s),), ("rot", s))
        ts(T.los[:, o:o + 128], T.rb[:, 0:128], T.tg[:, 8 + s:9 + s], BIG, ALU.is_equal, ALU.mult, 128, ("rb", "tl"), (("los", s),), 0.5)
    ts(T.b0[:], T.rb[:], G16, BIG, ALU.is_equal, ALU.mult, 144, ("rb", "g16"), ("b0",), 0.5)
    iota(T.ct[:, 0:144:3], [[-16, 3], [0, 16]], "ct0", 32)
    iota(T.ct[:, 1:96:3], [[-16, 2], [0, 16]], "ct1", 80)
    iota(T.ct[:, 2:48:3], [[0, 16]], "ct2", 64)
    iota(T.ct[:, 97:288:3], [[0, 64]], "ct3", int(BIG))
    iota(T.ct[:, 50:288:3], [[0, 80]], "ct4", int(BIG))
    iota(T.ct[:, 144:288:3], [[0, 48]], "ct5", 0)
    iota(T.rst2[:, 0:288:3], [[0, 96]], "rs0", int(NONE))
    iota(T.rst2[:, 1:288:3], [[0, 96]], "rs1", -16384)
    iota(T.rst2[:, 2:288:3], [[0, 96]], "rs2", -16384)
    slot[0] = 1.0
    for j in range(16):
        mark(T.seld[:, 128 * j:128 * j + 128], T.zero[:], [[-16, 8], [0, 16]], 1.0, -j, ("zero",), ("seld", j))
    phi = [("phi", q) for q in range(8)]
    for q in range(8):
        iota(T.ph[:, 390 * q:390 * q + 390], [[0, 390]], ("phi", q), 8)

    def hop(bank, out, e, n):
        return [(T[bank][32 * (c // 2):32 * (c // 2) + 32, out], T.sel[:, 16 - 16 * (c % 2):48 - 16 * (c % 2)], e(c)) + n(c)
                for c in range(8)]

    pcount = [0]

    def step(i, s, b):
        t = ST * i + s
        last = s == ST - 1
        nv = NV[i][s][b]
        W = 256 if last else 128
        vl, zr = T["vl%d" % i], T["zr%d" % i]
        nm, nf, pg, a1, a2, e1, pk = (T["%s%d" % (n, b)] for n in ("nm", "nf", "pg", "a1", "a2", "e1", "pk"))
        bank = "pk%d" % b
        lst = vl[:, NOFF[s] + 8 * b:NOFF[s] + 8 * b + 8]
        vn = ("vl", i, s, b)
        nzl = T.nzk[:, 128 * b + t:128 * b + t + 128]
        slot[0] = 2 * t + 1 - b - 2.0
        cp(nm[:], T.adjs[:, 0:V].indirect(lst), 128, ("adjs", vn), (("nm", b),), cost=_ga(128))
        slot[0] = 2 * t + 1 - b
        ts(nf[:], nm[:], 2048.0, None, ALU.subtract, None, 128, (("nm", b),), (("nf", b),), 0.5)
        mm([(pk[:, 0:W], nzl, T.i4k[:, 0:W], True, False)], ("nzk0", "nzk1", "i4k0", "i4k1"), (bank,))
        a1n = []
        cuts = [nv + 2 * ((128 - nv) * q // (2 * SPIECES)) for q in range(SPIECES + 1)]
        for c0, c1 in zip(cuts, cuts[1:]):
            n = 16 * (c1 - c0)
            pn = "pd%d" % (pcount[0] % 2)
            pcount[0] += 1
            pd = T[pn]
            n1, n2 = ("a1", b, pn), ("a2", b, pn)
            add("S", lambda c0=c0, c1=c1: sca.activation(a2[:, 16 * c0:16 * c1], T.xs[:, 0:V].indirect(nm[:, c0:c1]), ACT.Copy),
                10.0 + _ga(n), ("xs", ("nm", b)), (n2, ("a2", b, "v")) if c0 == 0 else (n2,))
            banks = [(o, min(n, o + 512)) for o in range(0, n, 512)]
            mm([(pd[:, o:e], T.ib[:], zr[:, 2048 * b + 16 * c0 + o:2048 * b + 16 * c0 + e], True, False) for o, e in banks], ["ib"] + zall[i], (pn,))
            mm([(pd[:, o:e], T.ib[:], a2[:, 16 * c0 + o:16 * c0 + e], False, True) for o, e in banks], ("ib", n2), (pn,))
            add("S", lambda c0=c0, c1=c1, pd=pd, n=n: sca.activation(a1[:, 16 * c0:16 * c1], pd[:, 0:n], ACT.Abs, scale=0.5),
                _v(n), (), (n1, ("a1", b, "v")) if c0 == 0 else (n1,), (pn,))
            a1n.append(n1)
        if nv:
            n = 16 * nv
            n1, n2 = ("a1", b, "v"), ("a2", b, "v")
            add("V", lambda: vec.tensor_tensor(a2[:, 0:n], T.xs[:, 0:V].indirect(nm[:, 0:nv]), zr[:, 2048 * b:2048 * b + n], ALU.add),
                _ga(n), ["xs", ("nm", b)] + zall[i], (n2,))
            ts(a1[:, 0:n], a2[:, 0:n], 0.0, None, ALU.max, None, n, (n2,), (n1,), 0.5)
            a1n.append(n1)
            mm([(pk[0:nv, k:W:16], a2[:, k:16 * nv:16], T.c2[:, 0:W // 16], False, False) for k in range(16)], (n2, "c2"), (bank,))
        k1, k2 = (128, 0) if last and b == 0 else (0, 128)
        if i >= 2:
            add("S", lambda: sca.activation(pg[:], T.ph[:, 0:V].indirect(lst), ACT.Copy), 10.0 + _ga(128), ("ph", vn), (("pg", b),))
        allw = [(n, b, q) for n in ("a1", "a2") for q in ("pd0", "pd1", "v")]
        mm([(pk[:, k:W:16], a1[:, k:2048:16], T.c1[:, 0:W // 16], False, False) for k in range(16)], allw + ["c1"], (bank,))
        fin, rd = [], [("nf", b), "ib", "i2", "nzk0", "nzk1"]
        if i >= 2:
            fin.append((pk[:, 0:W], pg[:], T.i65[:, 0:W], False, False))
            rd += [("pg", b), "i650", "i651", "i32"]
            if last:
                fin.append((pk[:, k2:k2 + 128], pg[:], T.i32[:], False, False))
        if last:
            fin.append((pk[:, k2:k2 + 128], nzl, T.i2[:], False, False))
        fin.append((pk[:, k1:k1 + 128], nf[:], T.ib[:], False, True))
        mm(fin, rd, (bank,))
        so = 512 + 256 * b if last else 256 * s + 128 * b
        sc, scn = T.sc[:, so:so + W], ("sc", s, b)
        add("V", lambda: vec.tensor_tensor_scan(sc, T.rst[:, 0:W], pk[:, 0:W], 0.0, ALU.add, ALU.max), _v(W), ("rst",), (scn,), (bank,))
        nq = W // 128
        wn = 24 * b
        ts(T.wn[:, wn:wn + 8 * nq], sc[:, 15:W:16], 4095, None, AND, None, 8, (scn,), ("wn%d" % b, "wd%d" % b))
        if last:
            kc, wd = T.k2[:, 8 * b:8 * b + 8], T.wn[:, wn + k2 // 16:wn + k2 // 16 + 8]
            ts(kc, sc[:, k2 + 15:k2 + 128:16], 11, None, ALU.arith_shift_right, None, 8, (scn,), (("k2", b),))
            tt(wd, wd, kc, ALU.subtract, 8, (("k2", b), "wd%d" % b), ("wd%d" % b,))
        el = T.el[:, 4:12] if last else T.el[:, 0:4]
        add("V", lambda: vec.tensor_scalar(e1[:, 0:64 * nq], T.wn[:, wn:wn + 24].indirect(el), CEN, None, ALU.subtract),
            _ga(64 * nq), ("wn%d" % b, "wd%d" % b, "el0"), (("e1", b),))

        def nodes():
            mm(hop(bank, slice(256, 256 + 8 * nq), lambda c: e1[:, 8 * nq * c:8 * nq * (c + 1)], lambda c: (c % 2 == 0, c % 2 == 1)),
               (("e1", b), "sel"), (bank,))
            o = 64 + 16 * b if last else NOFF[s + 1] + 8 * b
            ts(vl[:, o:o + 8 * nq], pk[:, 256:256 + 8 * nq], CEN, None, ALU.add, None, 8, (), (("vl", i, s + 1, b),), x=(bank,))
            if last and i < VIS - 1:
                send(nxt, vl[:, o:o + 16], T["vl%d" % (i + 1)][:, 8 + 16 * b:24 + 16 * b], "r_v%d%d" % (i + 1, b),
                     (("vl", i, 3, b),), (("vl", i + 1, 0, b),), 2100.0)

        def flags():
            dp, lst = T["nc%d" % i][:, 8 + 24 * b:16 + 24 * b], []
            for o in (272, 280, 288):
                lst.append((pk[:, o:o + 8], T.im1[:], dp, True, False))
                lst += hop(bank, slice(o, o + 8), lambda c: e1[:, 16 * c + k2 // 16:16 * c + k2 // 16 + 8], lambda c: (False, c % 2 == 1))
            mm(lst, (("e1", b), "sel", "im1", ("nc", i, 0)), (bank,))
            fo = T["fo%d" % i][:, 24 * b:24 * b + 24]
            ts(fo, pk[:, 272:296], 0.0, BIG, ALU.is_ge, ALU.mult, 24, (), (("fo", i, b),), x=(bank,))
            send(prv, fo, T["fb%d" % i][:, 24 * b:24 * b + 24], "r_f%d%d" % (i, b), (("fo", i, b),), (("fb", i, b),), 2100.0)
        for part in ((nodes,) if not last or i == 0 else (nodes, flags) if b == 1 and i < VIS - 1 else (flags, nodes)):
            part()

    def centre(i, q, lo, hi, r):
        ts(T["nc%d" % i][:, lo:hi], T["vl%d" % i][:, lo:hi], CEN, None, ALU.subtract, None, hi - lo, r, (("nc", i, q),), 0.5)

    def trails(i):
        slot[0] = 6 * i + 6.5
        nc, so, ul, dl, pb = T["nc%d" % i], T["so%d" % i], T["ul%d" % i], T["dl%d" % i], T.pe1
        ts(T.w2[:, 0:64], T.sc[:, 15:1024:16], 12, 15, SHR, AND, 64, [("sc", s, b) for s in range(3) for b in range(2)], ("w2k",))
        centre(i, 1, 48, 112, [("vl", i, s, b) for s in (1, 2, 3) for b in range(2)])
        slot[0] = 6 * i + 8.5
        cp(T.ek[:], T.w2[:, 0:72].indirect(T.el[:, 12:36]), 384, ("w2k", "el1"), ("ek",), cost=_ga(384))
        pairs = ("01", "12", "23", "02", "13", "03")
        lst = []
        for q, pr in enumerate(pairs):
            u, w = NOFF[int(pr[0])], NOFF[int(pr[1])]
            out = pb[:, 288 + 16 * q:304 + 16 * q]
            lst += [(out, T.ib[:], nc[:, u:u + 16], True, False), (out, T.im1[:], nc[:, w:w + 16], False, True)]
        mm(lst, (("nc", i, 0), ("nc", i, 1), "ib", "im1"), ("pe1",))
        ts(T.e[:], pb[:, 288:384], 0.0, None, ALU.is_equal, None, 96, (), ("e",), x=("pe1",))
        e = {pr: 16 * q for q, pr in enumerate(pairs)}
        mm([(pb[:, 0:288], T.ib[:], T.ct[:], True, False)], ["ib"] + ["ct%d" % q for q in range(6)], ("pe1",))
        for (p, cand, s, lift) in ((0, 0, 0, ()), (0, 1, 1, ("01",)), (0, 2, 2, ("02",)), (1, 0, 1, ()), (1, 1, 2, ("01", "12")), (2, 0, 2, ())):
            out = slice(48 * p + cand, 48 * p + 48, 3)
            mm(hop("pe1", out, lambda c: T.ek[:, 48 * c + 16 * s:48 * c + 16 * s + 16], lambda c: (False, False))
               + [(pb[:, out], T.im64[:], T.e[:, e[pr]:e[pr] + 16], False, False) for pr in lift], ("ek", "sel", "im64", "e"), ("pe1",))
        for b in range(2):
            for (p, cand, s, up, down) in ((0, 0, 0, ("03",), ()), (1, 0, 1, ("01", "02", "13", "03"), ()),
                                           (1, 1, 2, ("23", "02", "03"), ("01",)), (2, 0, 2, pairs, ())):
                o = 144 + 72 * b + 24 * p
                out = pb[:, o + cand:o + 24:3]
                lst = [(out, T.ib[:], nc[:, NOFF[s] + 8 * b:NOFF[s] + 8 * b + 8], False, False)]
                lst += [(out, T.im4k[:], T.e[:, e[pr] + 8 * b:e[pr] + 8 * b + 8], False, False) for pr in down]
                lst += [(out, T.i4k[:, 0:128], T.e[:, e[pr] + 8 * b:e[pr] + 8 * b + 8], False, b == 1 and p == 2 and pr == up[-1]) for pr in up]
                mm(lst, ("ib", "i4k0", "im4k", "e", ("nc", i, 0), ("nc", i, 1)), ("pe1",))
        add("V", lambda: vec.tensor_tensor_scan(so[:, 0:288], T.rst2[:], pb[:, 0:288], 0.0, ALU.max, ALU.min), _v(288),
            ("rs0", "rs1", "rs2"), (("so", i),), ("pe1",))
        ts(ul[:], so[:, 2:288:3], CEN, None, ALU.add, None, 96, (("so", i),), (("ul", i),), 0.5)
        add("S", lambda: sca.activation(dl[:], T.xs[:, V - int(CEN):V + 48].indirect(ul[:, 0:48]), ACT.Copy),
            10.0 + _ga(768), ("dtab", "xs", ("ul", i)), (("dl", i),))
        for b in (1, 0):
            o = 146 + 72 * b
            for q in range(4):
                lst = []
                for j in range(4 * q, 4 * q + 4):
                    out = pb[:, 192 * b + 12 * j:192 * b + 12 * j + 12]
                    lst += [(out, T.seld[:, 128 * j:128 * j + 128], so[:, o + 3:o + 72:6], True, False),
                            (out, T.im1[:], so[:, o:o + 72:6], False, True)]
                mm(lst, [("so", i), "im1"] + [("seld", j) for j in range(4 * q, 4 * q + 4)], ("pe1",))

    def reinforce(i):
        j0 = i - 1
        so, ul, dl = T["so%d" % j0], T["ul%d" % j0], T["dl%d" % j0]
        for b in (1, 0):
            slot[0] = 6 * i + 6.0 - b
            bk, o = "pe1", 24 * b
            pb, eq, fb = T[bk], T["eq%d" % b], T["fb%d" % i][:, o:o + 24]
            ub = so[:, 146 + 72 * b:218 + 72 * b:3]
            for first, rhs, r in ((True, ub, ("so", j0)), (False, fb, ("fb", i, b))):
                mm([(T.pe0[:, 24 * s:24 * s + 24], T.rot[:, 128 * s:128 * s + 128], rhs, first and s == 0, not first and s == 7)
                    for s in range(8)], [r] + [("rot", s) for s in range(8)], ("pe0",))
            for h in range(4):
                ts(eq[:, 192 + h:384:4], pb[:, 192 * b + h:192 * b + 192:4], fb[:, 2 * h:2 * h + 1], None, ALU.is_equal, None, 48,
                   (("fb", i, b),), (("eqx", b, h),), x=(bk,))
            ts(eq[:, 0:192], T.pe0[:, 0:192], 0.0, None, ALU.is_equal, None, 192, (), (("eq", b),), x=("pe0",))
            cnt = pb[:, 384:408]
            mm([(cnt, T.ib[:], ub, True, False), (cnt, T.ib[:], fb, False, False)]
               + [(pb[:, 385:408:2], T.b0[:, 16 - j:144 - j], eq[:, 192 + 12 * j:204 + 12 * j], False, False) for j in range(16)],
               [("eqx", b, h) for h in range(4)] + ["b0", "ib", ("fb", i, b), ("so", j0)], (bk,))
            mm([(cnt, T.los[:, 128 * s:128 * s + 128], eq[:, 24 * s:24 * s + 24], False, s == 7) for s in range(8)],
               [("eq", b)] + [("los", s) for s in range(8)], (bk,))
            ts(T.off[:, o:o + 24:2], pb[:, 384:408:2], DUC, CEN, ALU.min, ALU.add, 12, ("duc",), (("off0", b),), x=(bk,))
            ts(T.off[:, o + 1:o + 24:2], pb[:, 385:408:2], DUO, CEN, ALU.min, ALU.add, 12, ("duo",), (("off1", b),), x=(bk,))
        for p in range(3):
            slot[0] = 6 * i + (6.0 if p else 2.0)
            for b in (1, 0):
                c = 48 + 24 * b + 8 * p
                add("V", lambda p=p, b=b, c=c: vec.tensor_tensor(T.new[:, 128 * b:128 * b + 128], T.ph[:, 0:V + 48].indirect(ul[:, c:c + 8]),
                                                                 dl[:, 256 * p + 128 * b:256 * p + 128 * b + 128], ALU.add),
                    _ga(128), ["ph", ("ul", j0), ("dl", j0)] + phi, (("new", b),))
            for b in (1, 0):
                nw = T.new[:, 128 * b:128 * b + 128]
                ts(nw, nw, 0.0, 20.0, ALU.max, ALU.min, 128, (("new", b),), (("new", b),), 0.5)
            slot[0] = 6 * i + 6.0
            for h in range(14, -2, -2):
                c = 24 * (h // 8) + 8 * p + h % 8
                add("V", lambda c=c, h=h: vec.tensor_copy(T.ph[:, 0:V + 32].indirect(T.off[:, c:c + 2]), T.new[:, 16 * h:16 * h + 32]),
                    _ga(32, SCT), (("off0", h // 8), ("off1", h // 8), ("new", h // 8)), ("ph",))

    for i in range(VIS):
        slot[0] = 6 * i + 2.0
        if i < VIS - 1 or i > 0:
            centre(i, 0, 8 if i else 16, 40 if i else 32, (("vl", i, 0, 0), ("vl", i, 0, 1)))
        for s in range(ST):
            for b in (1, 0):
                step(i, s, b)
        if i + 2 < VIS:
            wishes(i + 2, (last_w["sends"],))
        if i >= 1:
            reinforce(i)
        if i < VIS - 1:
            trails(i)
    cp(T.yvs[:], T["vl%d" % (VIS - 1)][:, 72:88], 16, (("vl", VIS - 1, 3, 0), ("vl", VIS - 1, 3, 1)), ("yvs",))
    add("S", lambda: sca.dma_start(T.yv[:], T.yvs[:]), 100.0, ("yvs",), (), sem=("o_v", 16), lat=2000.0)
    add("Y", lambda: g.sync.dma_start(T.yp[:], T.ph[:, 0:V]), 100.0, ("ph",), (), sem=("o_p", 16), lat=4000.0)
    return ops, nsent[0]


def _place(ops, prio, pre):
    n = len(ops)
    st = [0.0] * n
    left = [len(p) for p in pre[0]]
    busy = {}
    heap = sorted((prio[k], k) for k in range(n) if not left[k])
    end = 0.0
    while heap:
        k = heap.pop(0)[1]
        t = pre[2][k]
        for d, lag in pre[0][k]:
            if st[d] + lag > t:
                t = st[d] + lag
        e, c = ops[k]["eng"], ops[k]["cost"]
        if e is not None:
            iv = busy.setdefault(e, [])
            j = len(iv)
            while j and iv[j - 1][1] > t:
                j -= 1
            while j < len(iv) and iv[j][0] < t + c:
                t = max(t, iv[j][1])
                j += 1
            iv.insert(j, (t, t + c))
        st[k] = t
        end = max(end, t + c + pre[3][k])
        for s in pre[1][k]:
            left[s] -= 1
            if not left[s]:
                it = (prio[s], s)
                lo, hi = 0, len(heap)
                while lo < hi:
                    m = (lo + hi) // 2
                    if heap[m] < it:
                        lo = m + 1
                    else:
                        hi = m
                heap.insert(lo, it)
    return st, end


SEED, ROUNDS, JIT, SHAKES, SWEEPS, WIN, MOVES, HOT, COLD, REACH = 1, 20, 500.0, 30000, 8, 300, 8000, 500.0, 50.0, 1.2


def _schedule(ops):
    n = len(ops)
    fw = ([[] for _ in ops], [[] for _ in ops], [0.0] * n, [o["lat"] for o in ops])
    bw = ([[] for _ in ops], [[] for _ in ops], [o["lat"] for o in ops], [0.0] * n)
    for k, o in enumerate(ops):
        for d, need in o["deps"].items():
            wake = 0.0 if o["eng"] is None else OWN if o["eng"] == ops[d]["eng"] else HOP
            lag = ops[d]["lat"] + wake if need else 0.0
            fw[0][k].append((d, ops[d]["cost"] + lag))
            fw[1][d].append(k)
            bw[0][d].append((k, o["cost"] + lag))
            bw[1][k].append(d)
    rng = np.random.default_rng(SEED)

    def back(st, z):
        rs, _ = _place(ops, [-(st[k] + ops[k]["cost"] + z[k]) for k in range(n)], bw)
        return [-(rs[k] + ops[k]["cost"]) for k in range(n)]
    best = None
    prio = [o["slot"] * 3200.0 + 0.001 * k for k, o in enumerate(ops)]
    for it in range(ROUNDS):
        st, end = _place(ops, prio, fw)
        if best is None or end < best[1]:
            best = (st, end)
        prio = back(best[0] if it % 4 == 3 else st, (rng.random(n) * (JIT if it % 2 else 0.0)).tolist())
    return _anneal(ops, sorted(range(n), key=lambda k: (best[0][k], k)), fw, rng)


def _anneal(ops, order, pre, rng):
    n = len(ops)
    names = sorted(set(o["eng"] for o in ops if o["eng"] is not None))
    eng = [names.index(o["eng"]) if o["eng"] is not None else -1 for o in ops]
    cost = [o["cost"] for o in ops]
    pred, succ = pre[0], pre[1]
    preds = [[d for d, lag in p] for p in pred]

    def run(seq, lo, free, st, by):
        free, who = free[:], [-1] * len(names)
        for k in seq[max(0, lo - 150):lo]:
            if eng[k] >= 0:
                free[eng[k]], who[eng[k]] = st[k] + cost[k], k
        for k in seq[lo:]:
            t, w = 0.0, -1
            for d, lag in pred[k]:
                x = st[d] + lag
                if x > t:
                    t = x
                    w = d
            e = eng[k]
            if e >= 0:
                if free[e] > t:
                    t = free[e]
                    w = -2 - who[e]
                free[e] = t + cost[k]
                who[e] = k
            st[k] = t
            by[k] = w
        return free

    def window(order, lo, hi, moves):
        st, by = [0.0] * n, [-1] * n
        free = run(order[:lo], 0, [0.0] * len(names), st, by)
        rest, behind = [0.0] * n, [0.0] * len(names)
        for k in reversed(order[hi:]):
            rest[k] = max(rest[k], cost[k] + ops[k]["lat"])
            if eng[k] >= 0:
                rest[k] = behind[eng[k]] = max(rest[k], cost[k] + behind[eng[k]])
            for d, lag in pred[k]:
                rest[d] = max(rest[d], lag + rest[k])
        seq = order[lo:hi]
        inside = set(seq)
        ends = [k for k in seq if rest[k] or not succ[k]]
        for k in ends:
            rest[k] = max(rest[k], cost[k] + ops[k]["lat"])

        def look(seq, a, st, by):
            last = run(seq, a, free, st, by)
            end, k = max([(st[k] + rest[k], k) for k in ends])
            for e, t in enumerate(last):
                if t + behind[e] > end and t > free[e]:
                    end, k = t + behind[e], [q for q in seq if eng[q] == e][-1]
            return end, k

        def chain(k, by):
            out = []
            d = by[k]
            while d != -1:
                if d < -1:
                    d = -2 - d
                    out.append((d, k))
                if d not in inside:
                    break
                k = d
                d = by[k]
            return out
        end, k = look(seq, 0, st, by)
        arcs, best, m = chain(k, by), (end, seq), len(seq)
        for it, r in enumerate(rng.random((moves, 4)).tolist()):
            if not arcs:
                break
            u, v = arcs[int(r[0] * len(arcs))]
            a, b = seq.index(u), seq.index(v)
            e, more, up = eng[u], int(-math.log(1.0 - r[2]) * REACH), r[1] < 0.5
            if up:
                while more and a > 0:
                    a -= 1
                    more -= eng[seq[a]] == e
                seg, mark, need = seq[a:b + 1], {v}, set(preds[v])
            else:
                while more and b < m - 1:
                    b += 1
                    more -= eng[seq[b]] == e
                seg, mark, need = seq[a:b + 1], {u}, set(succ[u])
            qs = set()
            for k in (seg[-2::-1] if up else seg[1:]):
                if k in need or eng[k] in qs:
                    mark.add(k)
                    need.update(preds[k] if up else succ[k])
                    if eng[k] != e and eng[k] >= 0:
                        qs.add(eng[k])
            if u in mark and v in mark:
                continue
            q2 = seq[:a] + [k for k in seg if (k in mark) == up] + [k for k in seg if (k in mark) != up] + seq[b + 1:]
            s2, b2 = st[:], by[:]
            e2, k = look(q2, a, s2, b2)
            if e2 <= end - HOT * (COLD / HOT) ** (it / moves) * math.log(1.0 - r[3]):
                seq, st, by, end = q2, s2, b2, e2
                arcs = chain(k, by)
                if it % 64 == 0:
                    seq = sorted(seq, key=lambda k: st[k])
                if end < best[0]:
                    best = (end, seq)
        return order[:lo] + best[1] + order[hi:], best[0]
    order, end = window(order, 0, n, SHAKES)
    for sweep in range(SWEEPS):
        for lo in range(-int(rng.random() * WIN / 2), n - WIN // 3, WIN // 2):
            order, end = window(order, max(0, lo), min(n, lo + WIN), MOVES)
    return order, None, window(order, 0, n, 0)[1]


_ORDER = {}


def rank_program(g, core, T, topo):
    rank = T.rank_of(core)
    if rank is None:
        return
    ops, nsent = _build(g, T, topo, core, rank)
    if "o" not in _ORDER:
        _ORDER["o"] = _schedule(ops)
    queue = {"V": g.vector, "S": g.scalar, "P": g.tensor, "G": g, "Y": g.sync}
    waited_on = set(d for o in ops if o["eng"] is not None for d, need in o["deps"].items() if need)
    count = {"V": 0, "S": 0, "P": 0, "G": 0}
    signal, total = {}, {}
    seen = {e: {} for e in queue}
    for k in _ORDER["o"][0]:
        o = ops[k]
        e = o["eng"]
        if e is None:
            signal[k] = o["sem"]
            total[o["sem"][0]] = o["sem"][1]
            continue
        want = {}
        for d, need in o["deps"].items():
            if need:
                nm, val = signal[d]
                want[nm] = max(want.get(nm, 0), val)
        for nm, val in want.items():
            if seen[e].get(nm, 0) < val:
                queue[e].wait_ge(T.sem[nm], val)
                seen[e][nm] = val
        ins = o["fn"]()
        if o["sem"] is not None:
            ins.then_inc(T.sem[o["sem"][0]], o["sem"][1])
            signal[k] = o["sem"]
            total[o["sem"][0]] = o["sem"][1]
        elif k in waited_on:
            count[e] += 1
            ins.then_inc(T.sem["c" + e], 1)
            signal[k] = ("c" + e, count[e])
            total["c" + e] = count[e]
    total["sent"] = nsent
    for nm, val in total.items():
        if seen["G"].get(nm, 0) < val:
            g.wait_ge(T.sem[nm], val)
